import numpy as np, ml_dtypes
CORES = [24,25,26,27,28,29,30,31]
N = 8
BF = ml_dtypes.bfloat16
V, NT, A, S, RO, CAP, VO, L = 4096, 64, 4, 7, 2, 96, 1024, 256
def parts(rng):
    par = np.zeros((N, 8, 16, NT), np.int64)
    for j in range(1, A): par[:, :, j] = rng.integers(0, j, (N, 8, NT))
    share = rng.choice(np.array([0.0, 0.3, 0.5, 0.7, 1.0]), (N, 8, 1, NT))
    return {"x": rng.integers(0, 256, (N, 8, 16, V)), "nb": rng.integers(0, V, (N, 8, 16, V)), "feat": rng.integers(0, 256, (N, 8, 16, (A - 1) * NT)), "chg": rng.integers(0, 256, (N, 8, 16, A * NT)),
            "par": par, "swp": (rng.random((N, 8, 16, NT)) < share).astype(np.int64), "wt": rng.integers(0, 64, (N, 8, 16, 1)), "beg": rng.integers(0, V, (N, 8, L)), "tau": rng.integers(0, NT, (N, 8, L))}
def limits(rng, p):
    base = np.array([650, 800, 950, 1100])[(np.arange(8)[None, :] + rng.integers(0, 4, (N, 1))) % 4]
    p["par"][:, :, 9:8 + A] = base[:, :, None, None] + rng.integers(0, 400, (N, 8, A - 1, NT))
    return p
def spell(rng, d):
    a = (d[None, :] + rng.permuted(np.tile(np.arange(16)[:, None], (1, V)), axis=0)) // 16
    t = np.floor(rng.random((8, V)) * (np.minimum(a[::2], 255 - a[1::2]) + 1)).astype(np.int64)
    a[::2] -= t; a[1::2] += t
    return a
def pack(p):
    o = {}
    for k in ("x", "nb", "feat", "chg", "par", "swp", "wt"):
        a = np.ascontiguousarray(p[k]).reshape(N, 128, -1)
        o[k] = a.astype(np.float32).astype(BF) if k in ("x", "feat", "chg", "swp") else a.astype(np.int32)
    o["beg"] = p["beg"].astype(np.int32); o["tau"] = p["tau"].astype(np.int32)
    return o
def setup_inputs(rng):
    return pack(limits(rng, parts(rng)))
def setup_inputs_brim(rng):
    p = parts(rng); p["x"] = np.minimum(p["x"], 254); h = V // 16
    for q in range(N):
        for g in range(8): p["nb"][q, g] = rng.permutation(16)[:, None] * h + rng.integers(0, h, (16, V))
    p["par"][:, :, 9:8 + A] = 4080; odd = np.arange(1, NT, 2); f = rng.integers(1, A, NT // 2)
    p["par"][:, :, 8 + f, odd] = 0; p["feat"][:, :, :, (f - 1) * NT + odd] = 255
    for q in range(N):
        for g in range(8):
            n = int(rng.choice(np.array([0, 1, CAP - 1, CAP, CAP + 1, L])))
            if q == 0: n = (CAP, CAP + 1, L, CAP - 1, 1, 0, CAP, CAP + 1)[g]
            if q == 1 and g < 2: n = CAP
            t = 2 * rng.integers(0, NT // 2, L); t[rng.permutation(L)[n:]] += 1; p["tau"][q, g] = t
    return pack(p)
def setup_inputs_clash(rng):
    p = parts(rng); p["par"][:, :, 9:8 + A] = rng.choice(np.array([4080, 1300]), (N, 8, 1, NT))
    for q in range(N):
        few = rng.permutation(V)[:64]; few[0] = 0; few[1] = V - 1
        p["nb"][q, 0] = few[rng.integers(0, 64, (16, V))]; p["beg"][q, 0] = few[rng.integers(0, 64, L)]
        a = p["tau"][q, 0, 0]; p["beg"][q, 0, 0] = V - 1; p["par"][q, 0, 9:8 + A, a] = 4080; p["swp"][q, 0, :, a] = 1
        p["nb"][q, 1] = p["nb"][q, 1, :1]
        for g in (2, 6): p["nb"][q, g] = np.where(rng.random((16, V)) < 0.5, np.arange(V)[None, :], p["nb"][q, g])
        s = rng.integers(0, V, 24); s[0] = 0; s[1] = V - 1; p["beg"][q, 3] = s[rng.integers(0, 24, L)]
        p["nb"][q, 4] = (V // 8) * rng.integers(0, 8, (16, V)); p["beg"][q, 4] = (V // 8) * rng.integers(0, 8, L)
        for g in (5, 7):
            o = rng.permutation(V); p["nb"][q, g, 0, o] = np.roll(o, -1)
            p["par"][q, g, 1:A] = np.arange(A - 1)[:, None]; p["par"][q, g, 9:8 + A] = 4080
            if g == 5:
                n = 256 // A; s = rng.integers(0, A, L); s[:n] = 0; s[n] = A - 256 % A; s[n + 1] = 0
                p["tau"][q, g] = int(p["tau"][q, g, 0])
            else: s = A * np.arange(L)
            p["beg"][q, g] = o[s % V]
    return pack(p)
def setup_inputs_ties(rng):
    p = parts(rng); p["x"] = rng.integers(0, 4, p["x"].shape); p["feat"] = rng.integers(0, 4, p["feat"].shape)
    p["chg"] = rng.choice(np.array([0, 1, 2, 255]), p["chg"].shape)
    p["par"][:, :, 9:8 + A] = rng.integers(12, 22, (N, 8, A - 1, NT))
    for q in range(N):
        two = rng.integers(0, 256, (16, 2)); p["x"][q, 1] = two[:, rng.integers(0, 2, V)]; p["feat"][q, 1] = two[:, rng.integers(0, 2, (A - 1) * NT)]
        p["par"][q, 1, 9:8 + A] = rng.choice(np.array([4080, 0]), (A - 1, NT))
        p["nb"][q, 1] = np.where(rng.random((16, V)) < 0.5, np.arange(V)[None, :], p["nb"][q, 1])
        for g, e in ((3, (2048, 2049, 2050, 2051, 2052)), (5, (3839, 3840, 3841, 3900, 4078, 4079, 4080))):
            t = np.array(e); s = spell(rng, np.minimum(t[rng.integers(0, len(e), V)] + rng.integers(-1, 2, V), 4080))
            m = rng.integers(0, 2 if g == 3 else 1, (16, 1))
            p["x"][q, g] = np.where(m == 1, 255 - s, s); p["feat"][q, g] = 255 * m
            p["par"][q, g, 9:8 + A] = t[rng.integers(0, len(e), (A - 1, NT))]
        p["wt"][q, 5] = rng.integers(60, 64, (16, 1))
    return pack(p)
def setup_inputs_walk(rng):
    p = limits(rng, parts(rng))
    for q in range(N):
        for g in range(0, 8, 2):
            v = np.zeros((A, NT), np.int64); v[0] = rng.integers(0, V, NT); v[0, 0] = 0; v[0, 1] = V - 1; a = np.arange(NT)
            for j in range(1, A):
                k = rng.integers(0, 16, NT); e = rng.random(NT); k = np.where(e < 0.25, 0, np.where(e < 0.5, 15, k))
                v[j] = p["nb"][q, g][k, v[p["par"][q, g, j], a]]
                p["feat"][q, g, :, (j - 1) * NT:j * NT] = p["x"][q, g][:, v[j]]; p["par"][q, g, 8 + j] = 0
            t = rng.permutation(np.arange(L) % NT); p["tau"][q, g] = t
            p["beg"][q, g] = np.where(rng.random(L) < 0.3, rng.integers(0, V, L), v[0][t])
    return pack(p)
def setup_inputs_spread(rng):
    p = parts(rng)
    for k in ("x", "feat", "chg"):
        s = p[k].shape; p[k] = np.floor(np.exp2(8 * rng.random((N, 8, 1, s[3]))) * rng.random(s)).astype(np.int64)
    e = rng.permuted(np.tile(np.array([0.5, 0.5, 1.0, 1.0, 2.0, 2.0, 4.0, 4.0]), (N, 1)), axis=1)
    p["par"][:, :, 9:8 + A] = np.minimum(np.floor(4081 * rng.random((N, 8, A - 1, NT)) ** e[:, :, None, None]), 4080).astype(np.int64)
    p["nb"] = np.floor(V * rng.random(p["nb"].shape) ** 2).astype(np.int64); p["beg"] = np.floor(V * rng.random((N, 8, L)) ** 3).astype(np.int64)
    p["wt"] = np.floor(np.exp2(6 * rng.random((N, 8, 16, 1))) * (0.5 + 0.5 * rng.random((N, 8, 16, 1)))).astype(np.int64)
    return pack(p)
def check_inputs(d):
    bad = []
    def test(k, a, lo, hi):
        a = np.asarray(a).astype(np.float64)
        if not (np.all(a >= lo) and np.all(a <= hi) and np.all(a == np.floor(a))): bad.append("range of " + k)
    for k, hi in (("x", 255), ("nb", V - 1), ("feat", 255), ("chg", 255), ("swp", 1), ("wt", 63), ("beg", V - 1), ("tau", NT - 1)): test(k, d[k], 0, hi)
    p = np.asarray(d["par"]).reshape(N, 8, 16, NT); rest = list(range(16))
    for j in range(1, A):
        test("parents in par", p[:, :, j], 0, j - 1); test("thresholds in par", p[:, :, 8 + j], 0, 4080); rest.remove(j); rest.remove(8 + j)
    test("other rows of par", p[:, :, rest], 0, 0)
    return bad
def reference(x, nb, feat, chg, par, swp, wt, beg, tau):
    B = N * 8; b = np.arange(B)[:, None]; b3 = b[:, :, None]; lane = np.arange(L); li = lane[None, :]
    def items(a, ty): return np.array(a.astype(np.float32).reshape(B, 16, -1).transpose(0, 2, 1), dtype=ty, order="C")
    X = items(x, np.int16); NB = items(nb, np.int32); F = items(feat, np.int16); C = items(chg, np.int16); P = items(par, np.int64); H = items(swp, np.int64) == 1
    W = wt.astype(np.int64).reshape(B, 1, 16); m0 = beg.astype(np.int64).reshape(B, L); T = tau.astype(np.int64).reshape(B, L)
    for rnd in range(RO):
        M = np.full((B, L, A), -1, np.int64); M[:, :, 0] = m0; K = np.zeros((B, L, A), np.int64); j = np.ones((B, L), np.int64)
        for step in range(S):
            jj = np.minimum(j, A - 1)
            c = NB[b, M[b, li, P[b, T, jj]]]
            dist = np.add.reduce(np.abs(X[b3, c] - F[b, (jj - 1) * NT + T][:, :, None, :]), axis=3, dtype=np.int32)
            good = (dist <= P[b, T, 8 + jj][:, :, None]) & (np.arange(16) >= K[b, li, jj][:, :, None])
            for i in range(A - 1): good &= (c != M[:, :, i:i + 1]) | (i >= jj)[:, :, None]
            found = np.any(good, axis=2); k = np.argmax(good, axis=2); ck = np.take_along_axis(c, k[:, :, None], 2)[:, :, 0]
            up = (j < A) & found; down = (j < A) & ~found
            bb, ll = np.nonzero(up); M[bb, ll, j[up]] = ck[up]; K[bb, ll, j[up]] = k[up] + 1
            j = np.where(up, j + 1, np.where(down, np.maximum(j - 1, 1), j))
            fresh = up & (j < A); bb, ll = np.nonzero(fresh); K[bb, ll, j[fresh]] = 0
        full = j == A; slot = np.argsort(~full, axis=1, kind="stable")[:, :CAP]
        got = np.take_along_axis(full, slot, 1); Ms = M[b, slot]; Ts = T[b, slot]
        same = np.any(Ms[:, :, None, :, None] == Ms[:, None, :, None, :], axis=(3, 4))
        lower = np.arange(CAP)[None, :] < np.arange(CAP)[:, None]
        go = got & ~np.any(same & lower & got[:, None, :], axis=2)
        bb, ss = np.nonzero(go); mm = Ms[bb, ss]; tt = Ts[bb, ss]; h = H[bb, tt]
        for i in range(0, A - 1, 2):
            p = NB[bb, mm[:, i]]; q = NB[bb, mm[:, i + 1]]
            NB[bb, mm[:, i]] = np.where(h, q, p); NB[bb, mm[:, i + 1]] = np.where(h, p, q)
        new = (X[bb[:, None], mm] + C[bb[:, None], np.arange(A)[None, :] * NT + tt[:, None]]) & 255
        X[bb[:, None], mm] = new
        Z = np.zeros((B, CAP, 16), np.int16); Z[bb, ss] = np.maximum.reduce(new, axis=1)
        Zr = Z.reshape(N, 8, CAP, 16); t = np.arange(CAP)
        come = np.stack([Zr[(r - 1 - t % (N - 1)) % N, :, t].transpose(1, 0, 2) for r in range(N)])
        u = np.add.reduce(X[b, M[b, li, j - 1]].astype(np.int64) * W, axis=2)
        u[:, :CAP] = np.add.reduce(come.reshape(B, CAP, 16).astype(np.int64) * W, axis=2)
        u = u & 4095
        T = (((u * u) >> 5) + li) & (NT - 1); m0 = (37 * u + li) & (V - 1)
    ym = np.where(np.arange(A)[None, None, :] < j[:, :, None], M, -1).transpose(0, 2, 1).reshape(N, 8, A * L)
    yx = X[:, :VO].transpose(0, 2, 1).reshape(N, 128, VO); yz = come.transpose(0, 1, 3, 2).reshape(N, 128, CAP)
    return {"yx": yx.astype(np.float32).astype(BF), "ym": ym.astype(np.float32), "yz": yz.astype(np.float32).astype(BF)}

@@ -1,0 +1,892 @@
+import numpy as np
+from concourse.bass import DstId, RemoteDMATransfer
+from concourse.mybir import AluOpType as ALU, ActivationFunctionType as ACT
+
+OFF = 512
+MID = OFF + 2048
+NW = 4096 + OFF
+SCRATCH = {
+    "nbi": ("sbuf", [128, 4096], "int32"),
+    "nbw": ("sbuf", [128, NW], "float32"),
+    "xw": ("sbuf", [128, NW], "bfloat16"),
+    "iow": ("sbuf", [128, NW], "float32"),
+    "sf": ("sbuf", [128, 14336], "float32"),
+    "sb": ("sbuf", [128, 36864], "bfloat16"),
+    "sh": ("sbuf", [128, 4096], "float16"),
+    "su": ("sbuf", [128, 2048], "uint16"),
+    "si": ("sbuf", [128, 1024], "int32"),
+    "land0": ("sbuf", [128, 112], "bfloat16"),
+    "land1": ("sbuf", [128, 112], "bfloat16"),
+}
+for _k in range(8):
+    SCRATCH["ps%d" % _k] = ("psum", [128, 512], "float32")
+NDMA = 40
+SEMAPHORES = ["cV", "cA", "cP", "cG", "arr0", "arr1", "loc0", "loc1"] + ["d%d" % _k for _k in range(NDMA)]
+
+COST = {"ga": 1.56, "sc": 3.8, "pe": 0.5, "lat": 100.0, "fix": 10.0}
+RANGE = [dict(COST, ga=1.15, sc=2.2), COST, dict(COST, ga=1.95, sc=5.4)]
+PLAN = ["FMMM", "MMMM"]
+LEADS = [2500.0, 3000.0, 3500.0, 4000.0]
+STEPS = 500
+BETA = [0.5]
+LAST = {}
+
+
+def build(T, rank, core, topo, XENG):
+    ops = []
+    hist = {}
+    tag = [None]
+    top = {"sf": 0, "sb": 0, "sh": 0, "su": 0, "si": 0}
+    size = {"sf": 4, "sb": 2, "sh": 2, "su": 2, "si": 4, "nbi": 4, "nbw": 4, "xw": 2, "iow": 4, "land0": 2, "land1": 2}
+
+    def al(buf, n):
+        a = top[buf]
+        top[buf] = a + (n + 15) // 16 * 16
+        return (buf, a, a + n, 1)
+
+    def sl(t, a, b, s=1):
+        n = (b - a + s - 1) // s
+        lo = t[1] + a * t[3]
+        return (t[0], lo, lo + (n - 1) * s * t[3] + 1, s * t[3])
+
+    def cnt(t):
+        return (t[2] - t[1] + t[3] - 1) // t[3]
+
+    def ap(t):
+        if len(t) == 2:
+            return ap(t[0]).indirect(ap(t[1]))
+        if t[3] == 1:
+            return T[t[0]][:, t[1]:t[2]]
+        return T[t[0]][:, t[1]:t[2]:t[3]]
+
+    def isps(t):
+        return t[0][:2] == "ps"
+
+    def tiles(xs):
+        r = []
+        for x in xs:
+            if isinstance(x, tuple):
+                if len(x) == 2:
+                    r += [x[0], x[1]]
+                else:
+                    r.append(x)
+        return r
+
+    def val(x):
+        return ap(x) if isinstance(x, tuple) else x
+
+    def add(eng, fn, reads, writes, cost, kind="c", hold=None, extra=(), sem=None):
+        i = len(ops)
+        deps = set(extra)
+        acc = [(t, False) for t in reads] + [(t, True) for t in writes]
+        for t, w in acc:
+            lo, hi = (0, 512) if isps(t) else (t[1], t[2])
+            w = w or isps(t)
+            for (j, l2, h2, w2, s2) in hist.get(t[0], []):
+                if (w or w2) and l2 < hi and lo < h2 and (isps(t) or s2 != t[3] or (lo - l2) % s2 == 0):
+                    deps.add(j)
+        for t, w in acc:
+            lo, hi = (0, 512) if isps(t) else (t[1], t[2])
+            w = w or isps(t)
+            h = hist.setdefault(t[0], [])
+            if w and (isps(t) or t[3] == 1):
+                h[:] = [e for e in h if not (lo <= e[1] and e[2] <= hi)]
+            h.append((i, lo, hi, w, t[3]))
+        deps.discard(i)
+        ops.append({"fn": {eng: fn}, "deps": sorted(deps), "cost": {eng: cost}, "kind": kind,
+                    "hold": {eng: cost if hold is None else hold}, "sem": sem, "tag": tag[0]})
+        return i
+
+    def vcost(out, ins, two=False):
+        if len(out) == 2:
+            return ("sc", 16 * cnt(out[1]))
+        for x in ins:
+            if isinstance(x, tuple) and len(x) == 2:
+                return ("ga", 16 * cnt(x[1]))
+        n = cnt(out)
+        ts_ = tiles([out] + ins)
+        if two:
+            return ("el", n * (1.0 if any(isps(t) for t in ts_[1:]) else 2.0))
+        return ("el", n * (0.5 if all((not isps(t)) and size[t[0]] == 2 for t in ts_) else 1.0))
+
+    def wr(out):
+        return ([out[1]], [out[0]]) if len(out) == 2 else ([], [out])
+
+    def tt(out, a, b, op):
+        r, w = wr(out)
+        return add("V", lambda q: q.tensor_tensor(ap(out), ap(a), ap(b), op), tiles([a, b]) + r, w, vcost(out, [a, b], True))
+
+    def ts(out, a, s1, s2, op0, op1=None):
+        r, w = wr(out)
+        if op1 is None:
+            f = lambda q: q.tensor_scalar(ap(out), ap(a), val(s1), None, op0)
+        else:
+            f = lambda q: q.tensor_scalar(ap(out), ap(a), val(s1), val(s2), op0, op1)
+        return add("V", f, tiles([a, s1, s2]) + r, w, vcost(out, [a]))
+
+    def cp(out, a):
+        r, w = wr(out)
+        return add("V", lambda q: q.tensor_copy(ap(out), ap(a)), tiles([a]) + r, w, vcost(out, [a]))
+
+    def ms(out, c):
+        return add("V", lambda q: q.memset(ap(out), c), [], [out], vcost(out, []))
+
+    def scan(out, d0, d1, init, op0, op1):
+        return add("V", lambda q: q.tensor_tensor_scan(ap(out), ap(d0), ap(d1), val(init), op0, op1),
+                   tiles([d0, d1, init]), [out], vcost(out, [d0, d1]))
+
+    def act(out, a, func, bias=None, scale=None):
+        kw = {}
+        if bias is not None:
+            kw["bias"] = val(bias)
+        if scale is not None:
+            kw["scale"] = val(scale)
+        c = ("ga", 16 * cnt(a[1])) if len(a) == 2 else ("el", float(cnt(out)))
+        return add("A", lambda q: q.activation(ap(out), ap(a), func, **kw), tiles([a, bias, scale]), [out], c)
+
+    def either(i, out, a, f):
+        ops[i]["fn"]["V"] = f
+        ops[i]["cost"]["V"] = vcost(out, [a])
+        ops[i]["hold"]["V"] = vcost(out, [a])
+
+    def move(out, a):
+        either(act(out, a, ACT.Copy), out, a, lambda q: q.tensor_copy(ap(out), ap(a)))
+
+    def relu(out, a, b=0.0):
+        either(act(out, a, ACT.Relu, bias=b), out, a, lambda q: q.tensor_scalar(ap(out), ap(a), val(b), 0.0, ALU.add, ALU.max))
+
+    def times(out, a, c):
+        either(act(out, a, ACT.Identity, scale=c), out, a, lambda q: q.tensor_scalar(ap(out), ap(a), val(c), None, ALU.mult))
+
+    def plus(out, a, c):
+        either(act(out, a, ACT.Identity, bias=c), out, a, lambda q: q.tensor_scalar(ap(out), ap(a), val(c), None, ALU.add))
+
+    def mm(lst):
+        def f(q):
+            r = None
+            for (o, l, rr, st, sp) in lst:
+                r = q.matmul(ap(o), ap(l), ap(rr), st, sp)
+            return r
+        c = sum(max(64, cnt(rr)) * (4 if size[rr[0]] == 4 else 1) for (o, l, rr, st, sp) in lst)
+        return add("P", f, tiles([x for m in lst for x in m[1:3]]), [m[0] for m in lst], ("pe", c))
+
+    def iota(out, pat, base, cm, flag=True):
+        if flag:
+            f = lambda q: q.iota(ap(out), pat, base, cm, allow_small_or_imprecise_dtypes=True)
+        else:
+            f = lambda q: q.iota(ap(out), pat, base, cm)
+        return add("G", f, [], [out], ("raw", 160 + 2 * cnt(out)))
+
+    def asel(out, a, pat, op, fill, base, cm):
+        return add("G", lambda q: q.affine_select(ap(out), ap(a), pat, op, fill, base, cm), [a], [out], ("raw", 200 + 2 * cnt(out)))
+
+    nd = [0]
+
+    def dma(eng, oap, iap, reads, writes, nbytes):
+        s = "d%d" % nd[0]
+        nd[0] += 1
+        return add(eng, lambda q: q.dma_start(oap, iap), reads, writes, ("raw", 2400 + nbytes / 200.0), kind="d", hold=("raw", 80), sem=s)
+
+    F = lambda n: al("sf", n)
+    B = lambda n: al("sb", n)
+    U = lambda n: al("su", n)
+    I = lambda n: al("si", n)
+    H = lambda n: al("sh", n)
+    PS = lambda k, a, b: ("ps%d" % k, a, b, 1)
+    half = lambda t, s: sl(t, 8 * s, 8 * s + 8)
+    nbw = ("nbw", 0, NW, 1)
+    xw = ("xw", 0, NW, 1)
+    iow = ("iow", 0, NW, 1)
+
+    begi, taui = I(16), I(16)
+    parA, parB, wti = I(64), I(64), I(16)
+    featw, chgw, swpw = B(208), B(256), B(256)
+    ms(parB, 0)
+    tload = 0
+    for c in range(4):
+        t = ("nbi", 1024 * c, 1024 * c + 1024, 1)
+        tload += 524288
+        dma("S", ap(t), T.nb[:, 1024 * c:1024 * c + 1024], [], [t], tload)
+        ts(sl(nbw, OFF + 1024 * c, OFF + 1024 * c + 1024), t, float(OFF), None, ALU.add)
+    for c in range(2):
+        t = sl(xw, OFF + 2048 * c, OFF + 2048 * c + 2048)
+        tload += 524288
+        dma("S", ap(t), T.x[:, 2048 * c:2048 * c + 2048], [], [t], tload)
+    for s in (1, 0):
+        dma("A", ap(half(taui, s)), T.tau[:, 128 * s:128 * s + 128], [], [half(taui, s)], 4096)
+        dma("A", ap(half(begi, s)), T.beg[:, 128 * s:128 * s + 128], [], [half(begi, s)], 4096)
+    dma("A", ap(parA), T.par[:], [], [parA], 32768)
+    dma("A", ap(sl(featw, 16, 208)), T.feat[:], [], [sl(featw, 16, 208)], 49152)
+    dma("A", T.si[0:125, parB[1]:parB[2]], T.par[3:128, :], [], [parB], 32768)
+    dma("S", ap(chgw), T.chg[:], [], [chgw], tload)
+    dma("S", ap(sl(swpw, 0, 64)), T.swp[:], [], [sl(swpw, 0, 64)], tload)
+    dma("S", ap(sl(wti, 0, 1)), T.wt[:], [], [wti], tload)
+    ms(sl(nbw, 0, OFF), 16.0)
+    ms(sl(xw, 0, OFF), 0.0)
+    ms(sl(xw, 16, 32), 8192.0)
+    ms(sl(featw, 0, 16), 0.0)
+
+    pi_, pki, tmpi = I(1), I(1), I(8)
+    pk = F(1)
+    iota(pi_, [[0, 1]], 0, 1, False)
+    ts(pki, pi_, 15, None, ALU.bitwise_and)
+    cp(pk, pki)
+    iota(sl(iow, 0, 512), [[1, 512]], -MID, 0)
+    for c in range(1, NW // 512):
+        plus(sl(iow, 512 * c, 512 * c + 512), sl(iow, 0, 512), float(512 * c))
+    BOf, ONE, IDf, ONEb = F(128), F(512), F(128), B(512)
+    ms(ONE, 1.0)
+    ms(ONEb, 1.0)
+    inblock = lambda o, a, n, fill: (asel(o, a, [[0, n], [-16, 8], [0, 16]], ALU.is_ge, fill, 0, 1),
+                                     asel(o, o, [[0, n], [16, 8], [0, 16]], ALU.is_ge, fill, 15, -1))
+    inblock(BOf, sl(ONE, 0, 128), 1, 0.0)
+    asel(IDf, sl(ONE, 0, 128), [[-1, 128]], ALU.is_equal, 0.0, 0, 1)
+    BO, NBO, ID, BIGI, N128I, TRI, TRI1 = B(128), B(128), B(128), B(128), B(128), B(128), B(128)
+    IDh = H(128)
+    move(BO, BOf)
+    times(NBO, BOf, -1.0)
+    move(ID, IDf)
+    cp(IDh, IDf)
+    times(BIGI, IDf, 8192.0)
+    times(N128I, IDf, -128.0)
+    asel(TRI1, BO, [[1, 128]], ALU.is_gt, 0.0, 0, -1)
+    trf = F(128)
+    times(trf, IDf, -8.0)
+    tt(trf, trf, TRI1, ALU.add)
+    times(TRI, trf, 4096.0)
+    SELN, SEL, WSEL = B(2048), B(2048), B(2048)
+    ms(SELN, -1.0)
+    asel(SELN, SELN, [[1, 128], [0, 16]], ALU.is_equal, 0.0, 0, -1)
+    io16, DEL, iob = F(128), F(128), B(128)
+    iota(io16, [[0, 8], [1, 16]], 0, 0)
+    iota(iob, [[0, 8], [1, 16]], 0, 0)
+    inblock(iob, iob, 1, -1.0)
+    for k in range(16):
+        ts(sl(SEL, 128 * k, 128 * k + 128), iob, float(k), None, ALU.is_equal)
+    SELf, SELh = F(128), H(640)
+    move(SELf, sl(SEL, 384, 512))
+    cp(SELh, sl(SEL, 0, 640))
+    wtf = F(1)
+    cp(wtf, sl(wti, 0, 1))
+    for k in range(4):
+        times(sl(WSEL, 512 * k, 512 * k + 512), sl(SEL, 512 * k, 512 * k + 512), wtf)
+    ts(DEL, io16, pk, None, ALU.is_equal)
+    dcol = lambda k: sl(DEL, k, k + 1)
+    DM = B(512)
+    for r in range(4):
+        ts(sl(DM, 128 * r, 128 * r + 128), DEL, float(2 ** 20 - 4096 * r * (r + 1)), float(-2 ** 20), ALU.mult, ALU.add)
+    SEGM, SEG6, SEG8, SEG4f, SEG4, SEGb = F(384), F(48), F(16), F(384), B(384), B(512)
+    asel(SEGM, sl(ONE, 0, 384), [[0, 24], [1, 16]], ALU.is_gt, 0.0, 0, 0)
+    asel(SEG6, sl(ONE, 0, 48), [[0, 8], [1, 6]], ALU.is_gt, 0.0, 0, 0)
+    asel(SEG8, sl(ONE, 0, 16), [[0, 2], [1, 8]], ALU.is_gt, 0.0, 0, 0)
+    asel(SEG4f, sl(ONE, 0, 384), [[0, 96], [1, 4]], ALU.is_gt, 0.0, 0, 0)
+    asel(SEG4, sl(ONEb, 0, 384), [[0, 96], [1, 4]], ALU.is_gt, 0.0, 0, 0)
+    nf = [XENG[0].count("F"), XENG[1].count("F")]
+    if nf[0] + nf[1] > 0:
+        asel(SEGb, ONEb, [[0, 32], [1, 16]], ALU.is_gt, 0.0, 0, 0)
+    WB = F(4)
+    for r in range(4):
+        ts(sl(WB, r, r + 1), pk, -4096.0, float(MID - 32768 + 8192 * r), ALU.mult, ALU.add)
+    thrw, codw = B(208), B(80)
+    hiA, loB = I(64), I(64)
+    ta, tb, ccol = F(64), F(64), F(1)
+    ms(sl(thrw, 0, 16), -1.0)
+    ms(sl(codw, 0, 16), 0.0)
+    ts(hiA, parA, 4080, None, ALU.bitwise_and)
+    ts(loB, parB, 15, None, ALU.bitwise_and)
+    for j in range(1, 4):
+        ts(ta, hiA, dcol(8 + j), None, ALU.mult)
+        ts(tb, loB, dcol(5 + j), None, ALU.mult)
+        tt(sl(thrw, 16 + 64 * (j - 1), 16 + 64 * j), ta, tb, ALU.add)
+    ts(ccol, dcol(3), 2.0, dcol(2), ALU.mult, ALU.add)
+    ts(sl(codw, 16, 80), parA, ccol, None, ALU.mult)
+    move(sl(swpw, 64, 128), sl(swpw, 0, 64))
+    move(sl(swpw, 128, 256), sl(swpw, 0, 128))
+    AQ, AT, AQh, ATh, RSh, gofs = F(512), F(512), H(512), H(512), H(512), F(1)
+    asel(AQ, ONE, [[4, 4], [-16, 8], [-1, 16]], ALU.is_equal, 0.0, 0, 1)
+    asel(AQ, AQ, [[0, 4], [-16, 8], [0, 16]], ALU.is_ge, 0.0, 0, 1)
+    asel(AQ, AQ, [[0, 4], [16, 8], [0, 16]], ALU.is_ge, 0.0, 3, -1)
+    asel(AT, ONE, [[0, 4], [-16, 8], [0, 16]], ALU.is_equal, 0.0, -4, 1)
+    asel(AT, AT, [[-4, 4], [0, 8], [1, 16]], ALU.is_ge, 0.0, 0, 0)
+    asel(AT, AT, [[4, 4], [0, 8], [-1, 16]], ALU.is_ge, 0.0, 3, 0)
+    cp(AQh, AQ)
+    cp(ATh, AT)
+    for i in range(4):
+        ts(sl(RSh, 128 * i, 128 * i + 128), BOf, dcol(i), None, ALU.mult)
+    ts(gofs, dcol(4), float(MID), float(-MID), ALU.mult, ALU.add)
+    c64, rofs = F(1), F(1)
+    ts(rofs, dcol(3), float(-MID), None, ALU.mult)
+    ts(sl(tmpi, 1, 2), pi_, 3, None, ALU.bitwise_and)
+    ts(c64, sl(tmpi, 1, 2), 64.0, None, ALU.mult)
+    w0, w1, w2, wcol, thr96, q8, q2, zer = F(1), F(1), F(1), F(24), F(96), F(24), F(96), F(96)
+    ts(sl(tmpi, 2, 3), pi_, 2, 1, ALU.logical_shift_right, ALU.bitwise_and)
+    ts(sl(tmpi, 3, 4), pi_, 3, 1, ALU.logical_shift_right, ALU.bitwise_and)
+    ts(w0, sl(tmpi, 2, 3), -0.75 * 2.0 ** 96, 2.0 ** 96, ALU.mult, ALU.add)
+    ts(w1, sl(tmpi, 3, 4), -0.9375, 1.0, ALU.mult, ALU.add)
+    tt(w2, w0, w1, ALU.mult)
+    ms(q8, 2.0 ** -8)
+    ms(q2, 0.25)
+    ms(zer, 0.0)
+    scan(wcol, q8, sl(zer, 0, 24), w2, ALU.mult, ALU.add)
+    scan(thr96, q2, zer, 7.0 * 2.0 ** 90, ALU.mult, ALU.add)
+    ioc, iol = F(24), F(16)
+    iota(ioc, [[1, 24]], 0, 0)
+    iota(iol, [[128, 2], [1, 8]], 0, 0)
+    lanef, dum16, neg16, n24, dum24, pk8, pk7 = F(16), F(16), F(16), F(24), F(24), F(1), F(1)
+    ts(pk8, pk, 8.0, None, ALU.mult)
+    ts(lanef, iol, pk8, None, ALU.add)
+    ts(dum16, lanef, 256.0, None, ALU.add)
+    ts(neg16, lanef, -1.0, -257.0, ALU.mult, ALU.add)
+    ts(n24, ioc, 16.0, pk, ALU.mult, ALU.add)
+    ts(dum24, n24, 64.0, None, ALU.add)
+    t6, q6, o6, r6 = F(6), I(6), F(6), F(6)
+    Lout, Lin = U(8), U(6)
+    ts(pk7, pk, 7.0, None, ALU.mult)
+    ts(Lout, sl(ioc, 0, 8), pk7, 95.0, ALU.add, ALU.min)
+    ts(r6, sl(n24, 0, 6), -3.0, 1.0 / 7.0, ALU.add, ALU.mult)
+    cp(q6, r6)
+    ts(t6, q6, -111.0, None, ALU.mult)
+    ts(o6, sl(n24, 0, 6), 16.0, None, ALU.mult)
+    tt(o6, o6, t6, ALU.add)
+    cp(Lin, o6)
+
+    FM, M3, Ew = F(64), F(16), H(1024)
+    LM0, LQ1, LQ2, LQ3 = U(16), U(16), U(16), U(16)
+    Q2e, Q3e, C2, U2, K30, w32 = F(16), F(16), F(16), F(16), F(16), F(16)
+    w21, w31, codi = I(16), I(16), I(16)
+    codg = B(256)
+    st = []
+    for s in range(2):
+        Z = F(320)
+        ms(Z, 0.0)
+        d = {"cu": U(128), "ch": H(128), "ft": [(B(128), B(128), B(128)) for _ in range(4)],
+             "eq": [B(128), B(128), B(128)], "xg": B(2048), "D": B(2048), "sg": B(128), "W": F(512),
+             "NS": [F(512), F(384), F(256), F(128), F(128)], "S": [sl(Z, 0, 56), sl(Z, 64, 120), sl(Z, 128, 184)],
+             "dl": F(48), "G": F(48), "tm": F(48), "Gz": [sl(Z, 192, 240), sl(Z, 256, 304)], "L": [F(24), F(24), F(24), F(24)],
+             "LPQ": U(24), "LM1": U(8), "dif": F(24), "Bq": F(16), "B1": F(8), "t": [F(8) for _ in range(8)], "g4": F(8)}
+        if nf[s] > 0:
+            d["Fz"], d["Fb"] = B(512 * nf[s]), B(1024)
+            ms(d["Fz"], 0.0)
+        st.append(d)
+    Rr, Gw, Gh = F(256), F(768), H(96)
+    hh, hb, sc_, a1, Y = F(16), F(16), B(16), F(16), F(64)
+    Lsl, LI, LC, Lsc, Lml = U(16), U(24), U(24), U(24), U(16)
+    If, dI, of = F(24), F(24), F(24)
+    rep = U(384)
+    eqb = B(4800)
+    okh = H(96)
+    xc, cc, sgn, new, zm, zz, zs, come, xl = B(384), B(384), B(384), B(384), B(384), B(96), B(128), B(96), B(256)
+    g0, gd, hs = F(384), F(384), B(384)
+    ui, sq, m0i, Ti = I(16), I(16), I(16), I(16)
+    ml = [F(16), F(16), F(16)]
+
+    def feats(s, lq, Fg, FT, Tg):
+        ex = 4 + s
+        move(Fg, (featw, lq))
+        mm([(PS(ex, 0, 128), Fg, ID, True, True)])
+        move(FT, PS(ex, 0, 128))
+        move(Tg, (thrw, lq))
+
+    def evaluate(s, e, lp, lq, cmps):
+        d = st[s]
+        R = 4 - e if e < 4 else 1
+        sb_, ex = 6 + s, 4 + s
+        cp(d["cu"], (nbw, lp))
+        ts(d["ch"], d["cu"], float(-MID), None, ALU.add)
+        Fg, FT, Tg = d["ft"][[0, 1, 3, 3, 2][e]]
+        if lq is not None:
+            feats(s, lq, Fg, FT, Tg)
+        if nf[s] > 0:
+            move(sl(d["Fz"], 0, 512 * nf[s], 16), sl(Fg, 0, 32 * nf[s]))
+        for i, lm in enumerate(cmps):
+            tt(d["eq"][i], (iow, lm), d["ch"], ALU.is_equal)
+        mm([(PS(sb_, 0, 128), NBO, Tg, True, False)])
+        for c in range(4):
+            xg = sl(d["xg"], 512 * c, 512 * c + 512)
+            src = (xw, sl(d["cu"], 32 * c, 32 * c + 32))
+            D = sl(d["D"], 512 * c, 512 * c + 512)
+            if XENG[s][c] == "F":
+                Fb = sl(d["Fb"], 512 * (c % 2), 512 * (c % 2) + 512)
+                scan(Fb, SEGb, sl(d["Fz"], 512 * c, 512 * c + 512), 0.0, ALU.mult, ALU.add)
+                tt(xg, src, Fb, ALU.subtract)
+                act(D, xg, ACT.Abs)
+            else:
+                bank = PS(2 * s + c % 2, 0, 512)
+                move(xg, src)
+                mm([(bank, FT, sl(SELN, 512 * c, 512 * c + 512), True, False)])
+                mm([(bank, ID, xg, False, True)])
+                act(D, bank, ACT.Abs)
+            if c % 2 == 1:
+                h = c // 2
+                if h == 1:
+                    mm([(PS(sb_, 0, 128), BIGI, d["eq"][i], False, False) for i in range(len(cmps))])
+                mm([(PS(sb_, 64 * h, 64 * h + 64), sl(SEL, 128 * k, 128 * k + 128), sl(d["D"], 1024 * h + k, 1024 * h + 1024, 16),
+                     False, h == 1 and k == 15) for k in range(16)])
+        act(d["sg"], PS(sb_, 0, 128), ACT.Sign, bias=-0.5)
+        X = PS(sb_, 128, 256)
+        mm([(X, IDh, d["ch"], True, False), (X, TRI, d["sg"], False, True)])
+        NS = d["NS"][e]
+        for r in range(R):
+            W = sl(d["W"], 128 * r, 128 * r + 128)
+            relu(W, X, sl(WB, r, r + 1))
+            if r == 0:
+                o = PS(ex if e < 4 else 2 * s, 0, 128)
+                mm([(o, ID, sl(DM, 0, 128), True, False)])
+                mm([(o, BOf, W, False, True)])
+                scan(sl(NS, 0, 128), sl(SEGM, 0, 128), o, 0.0, ALU.mult, ALU.max)
+        if R > 1:
+            o = PS(ex, 128, 512) if e == 0 else PS(sb_, 256, 128 + 128 * R)
+            mm([(o, ID, sl(DM, 128, 128 * R), True, False)])
+            for r in range(1, R):
+                mm([(sl(o, 128 * r - 128, 128 * r), BOf, sl(d["W"], 128 * r, 128 * r + 128), False, r == R - 1)])
+            scan(sl(NS, 128, 128 * R), sl(SEGM, 0, 128 * (R - 1)), o, 0.0, ALU.mult, ALU.max)
+            V = sl(NS, 15, 128 * R, 16)
+            tt(sl(d["dif"], 0, 8 * (R - 1)), sl(V, 8, 8 * R), sl(V, 0, 8 * (R - 1)), ALU.subtract)
+        return sl(NS, 15, 128, 16)
+
+    def search(s):
+        d = st[s]
+        hf = lambda t: half(t, s)
+        fld = lambda S, k: sl(S, k, 48, 6)
+        t = d["t"]
+        LP, LQ, LM2 = sl(d["LPQ"], 0, 8), sl(d["LPQ"], 8, 16), sl(d["LPQ"], 16, 24)
+        L = d["L"]
+
+        def prep(S, both):
+            tt(t[0], hf(w31), fld(S, 2), ALU.mult)
+            tt(fld(S, 0), t[0], hf(K30), ALU.add)
+            if both:
+                tt(t[1], hf(C2), fld(S, 3), ALU.mult)
+                tt(fld(S, 1), t[1], hf(U2), ALU.min)
+            tt(d["dl"], sl(S, 0, 48), sl(S, 1, 49), ALU.subtract)
+
+        def trans(S, S2, Gz, Bh, Lx, both):
+            ts(fld(Gz, 0), Bh, 1.0, None, ALU.min)
+            tt(t[2], hf(w32), Bh, ALU.mult)
+            tt(t[3], hf(Q2e), Bh, ALU.max)
+            scan(d["G"], SEG6, Gz, 0.0, ALU.mult, ALU.add)
+            tt(sl(Lx, 8, 16), t[3], hf(Q3e), ALU.min)
+            tt(d["tm"], d["G"], d["dl"], ALU.mult)
+            tt(sl(S2, 0, 48), d["tm"], sl(S, 1, 49), ALU.add)
+            tt(sl(Lx, 0, 8), t[2], fld(S2, 0), ALU.add)
+            if both:
+                cp(sl(d["LPQ"], 0, 16), sl(Lx, 0, 16))
+                cp(LM2, Bh)
+            else:
+                cp(d["LPQ"], Lx)
+            cp(d["LM1"], fld(S2, 2))
+            prep(S2, both)
+
+        def mixed(N0, is3, M2, B1, Bh):
+            tt(t[5], M2, B1, ALU.subtract)
+            tt(t[6], is3, N0, ALU.mult)
+            tt(t[0], N0, B1, ALU.add)
+            ts(t[7], t[6], 1.0, None, ALU.min)
+            tt(t[1], t[0], t[6], ALU.subtract)
+            tt(t[7], t[7], t[5], ALU.mult)
+            tt(Bh, t[1], t[7], ALU.add)
+
+        S = d["S"]
+        for k, lq in enumerate((LQ1, LQ2, LQ3)):
+            feats(s, hf(lq), d["ft"][k][0], d["ft"][k][1], d["ft"][k][2])
+        N0 = evaluate(s, 0, hf(LM0), None, [hf(LM0)])
+        tt(t[2], hf(C2), N0, ALU.mult)
+        tt(sl(L[0], 0, 8), t[2], hf(U2), ALU.min)
+        cp(LP, sl(L[0], 0, 8))
+        cp(d["LM1"], N0)
+        move(fld(S[0], 2), N0)
+        for r in range(3):
+            relu(fld(S[0], 3 + r), sl(d["dif"], 8 * r, 8 * r + 8))
+        prep(S[0], True)
+        N0 = evaluate(s, 1, LP, None, [hf(LM0), d["LM1"]])
+        trans(S[0], S[1], d["Gz"][0], N0, L[1], True)
+        relu(d["Bq"], sl(d["dif"], 0, 16))
+        M2 = N0
+        N0 = evaluate(s, 2, LP, LQ, [hf(LM0), d["LM1"], LM2])
+        is3 = fld(d["Gz"][0], 0)
+        B3 = sl(L[2], 16, 24)
+        mixed(N0, is3, M2, sl(d["Bq"], 0, 8), B3)
+        trans(S[1], S[2], d["Gz"][1], B3, L[2], False)
+        relu(t[5], sl(d["dif"], 0, 8))
+        tt(t[6], t[5], is3, ALU.mult)
+        tt(t[5], t[5], sl(d["Bq"], 8, 16), ALU.add)
+        tt(d["B1"], t[5], t[6], ALU.subtract)
+        N0 = evaluate(s, 3, LP, LQ, [hf(LM0), d["LM1"], LM2])
+        Bh = hf(sl(FM, 32, 48))
+        mixed(N0, fld(d["Gz"][1], 0), B3, d["B1"], Bh)
+        tt(t[2], hf(w32), Bh, ALU.mult)
+        tt(sl(L[3], 0, 8), t[2], fld(S[2], 0), ALU.add)
+        cp(LP, sl(L[3], 0, 8))
+        cp(LM2, Bh)
+        ts(d["g4"], Bh, 1.0, None, ALU.min)
+        tt(t[3], d["g4"], fld(d["dl"], 2), ALU.mult)
+        tt(hf(sl(FM, 16, 32)), t[3], fld(S[2], 3), ALU.add)
+        return LP
+
+    def lanes(s, mi, ti):
+        hf = lambda t: half(t, s)
+        M0 = hf(sl(FM, 0, 16))
+        ts(hf(LM0), hf(mi), float(OFF), None, ALU.add)
+        ts(hf(LQ1), hf(ti), 16.0, None, ALU.add)
+        ts(hf(LQ2), hf(ti), 80.0, None, ALU.add)
+        ts(hf(LQ3), hf(ti), 144.0, None, ALU.add)
+        ts(M0, hf(mi), float(OFF), None, ALU.add)
+        ts(hf(sl(FM, 48, 64)), hf(ti), float(MID), None, ALU.add)
+        plus(hf(Q2e), hf(sl(FM, 48, 64)), 80.0 - MID)
+        plus(hf(Q3e), hf(sl(FM, 48, 64)), 144.0 - MID)
+        cg = sl(codg, 128 * s, 128 * s + 128)
+        move(cg, (codw, hf(LQ1)))
+        o = PS(6 + s, 0, 8)
+        mm([(o, sl(SEL, 128 * a, 128 * a + 128), sl(cg, a, 128, 16), a == 0, a == 15) for a in range(16)])
+        cp(hf(codi), o)
+        ts(hf(w21), hf(codi), 1, None, ALU.bitwise_and)
+        ts(hf(w31), hf(codi), 1, 1, ALU.logical_shift_right, ALU.bitwise_and)
+        ts(hf(w32), hf(codi), 3.5, None, ALU.is_gt)
+        ts(hf(C2), hf(w21), -15.0, 16.0, ALU.mult, ALU.add)
+        ts(hf(U2), hf(w21), 8192.0, None, ALU.mult)
+        tt(hf(U2), hf(U2), M0, ALU.add)
+        ts(hf(K30), hf(codi), 1.5, None, ALU.is_lt)
+        tt(hf(K30), hf(K30), M0, ALU.mult)
+
+    N = len(T.cores)
+    mi, ti = begi, taui
+    for rnd in range(2):
+        last = rnd == 1
+        lps = []
+        for s in range(2):
+            tag[0] = s
+            lanes(s, mi, ti)
+            lps.append(search(s))
+        tag[0] = None
+        for a in range(16):
+            ts(sl(Ew, a, 1024, 16), FM, float(-MID), dcol(a), ALU.add, ALU.mult)
+        for s in range(2):
+            tag[0] = s
+            d = st[s]
+            o = PS(4 + s, 0, 128)
+            N0 = evaluate(s, 4, lps[s], None, [half(LM0, s), d["LM1"], sl(d["LPQ"], 16, 24)])
+            tt(half(M3, s), d["g4"], N0, ALU.mult)
+            tag[0] = None
+            for f in range(4):
+                k = f if f < 3 else 4
+                mm([(o, sl(SELh, 128 * k, 128 * k + 128), sl(Ew, 256 * f + 128 * s, 256 * f + 128 * s + 128), f == 0, False)])
+            mm([(o, SELf, sl(d["W"], 0, 128), False, True)])
+            plus(sl(Rr, 128 * s, 128 * s + 128), o, rofs)
+        if not last:
+            ms(sl(Gw, 96, 768), 0.0)
+        plus(sl(Gw, 0, 96), zer, gofs)
+        ts(hh, M3, 1.0, None, ALU.min)
+        scan(sc_, SEG8, hh, 0.0, ALU.mult, ALU.add)
+        tt(hb, hh, neg16, ALU.mult)
+        tt(hb, hb, dum16, ALU.add)
+        mm([(PS(6, 0, 2), TRI1, sl(sc_, 7, 16, 8), True, False), (PS(6, 1, 2), BO, sl(sc_, 7, 8), False, True)])
+        tt(a1, sc_, hb, ALU.add)
+        for s in range(2):
+            ts(half(Lsl, s), half(a1, s), PS(6, s, s + 1), None, ALU.add)
+        cp((Gw, Lsl), Rr)
+        cp(Gh, sl(Gw, 0, 96))
+        mm([(("ps3", i, 381 + i, 4), sl(RSh, 128 * i, 128 * i + 128), Gh, True, True) for i in range(4)])
+        wrap = lambda o, M, src: mm([(o, sl(M, 128 * q, 128 * q + 128), sl(src, q, 96, 4), q == 0, q == 3) for q in range(4)])
+        wrap(PS(7, 0, 24), AQh, Gh)
+        wrap(PS(6, 0, 24), ATh, Gh)
+        plus(If, PS(7, 0, 24), float(MID))
+        cp(LI, If)
+        ts(LC, PS(6, 0, 24), c64, None, ALU.add)
+        ts(rep, PS(3, 0, 384), float(MID), None, ALU.add)
+        move(xc, (xw, LI))
+        move(cc, (chgw, LC))
+        mm([(PS(0, 0, 384), ID, xc, True, False), (PS(0, 0, 384), ID, cc, False, True)])
+        act(sgn, PS(0, 0, 384), ACT.Sign, bias=-255.5)
+        mm([(PS(1, 0, 384), ID, xc, True, False), (PS(1, 0, 384), ID, cc, False, False), (PS(1, 0, 384), N128I, sgn, False, True)])
+        plus(new, PS(1, 0, 384), -128.0)
+        pos = 0
+        for j0 in range(0, 24, 3):
+            lst = []
+            for j in range(j0, j0 + 3):
+                w = 384 - 16 * j
+                e = sl(eqb, pos, pos + w)
+                pos += w
+                ts(e, sl(rep, 16 * j, 384), sl(If, j, j + 1), sl(wcol, j, j + 1), ALU.is_equal, ALU.mult)
+                lst.append((PS(2, 16 * j, 384), BO, e, j == 0, j == 23))
+            mm(lst)
+        tt(dI, If, dum24, ALU.subtract)
+        scan(zm, SEG4, new, 0.0, ALU.mult, ALU.max)
+        scan(PS(0, 0, 384), SEG4f, PS(2, 0, 384), 0.0, ALU.mult, ALU.add)
+        tt(okh, ("ps0", 3, 384, 4), thr96, ALU.is_lt)
+        tt(zz, sl(zm, 3, 384, 4), okh, ALU.mult)
+        cp(sl(zs, 0, 112), (zz, sl(Lout, 0, 7)))
+        land = ("land%d" % rnd, 0, 112, 1)
+
+        def send(q, rnd=rnd, land=land):
+            trs = []
+            for dd in range(N - 1):
+                dst = T.cores[(rank + 1 + dd) % N]
+                rid, pid, _ = topo.addr(dst)
+                en = topo.engines(core, dst)
+                k = len(en) // N
+                mask = sum(1 << x for x in en[k * dd:k * dd + k])
+                trs.append(RemoteDMATransfer(dst_ids=[DstId(rid=rid, pnc=pid)], dma_engine_mask=mask, remote_sem=T.sem["arr%d" % rnd],
+                                             src=ap(sl(zs, 16 * dd, 16 * dd + 16)), dst=ap(sl(land, 16 * dd, 16 * dd + 16))))
+            return q.remote_dma_fused(trs, local_sem=T.sem["loc%d" % rnd])
+        nsig = (N - 1) * (len(topo.engines(core, T.cores[(rank + 1) % N])) // N)
+        snd = add("G", send, [sl(zs, 0, 112)], [], ("raw", 1500), kind="r", hold=("raw", 600), sem=("loc%d" % rnd, nsig))
+        add("X", None, [], [land], ("raw", 3500), kind="x", extra=[snd], sem=("arr%d" % rnd, nsig))
+        wrap(PS(3, 0, 24), ATh, okh)
+        tt(of, PS(3, 0, 24), dI, ALU.mult)
+        tt(of, of, dum24, ALU.add)
+        cp(Lsc, of)
+        cp((xw, Lsc), new)
+        move(come, (land, Lin))
+        if last:
+            ts(sl(Y, 0, 32), sl(FM, 0, 32), float(-OFF), -1.0, ALU.add, ALU.max)
+            tt(ml[0], sl(FM, 32, 48), hh, ALU.mult)
+            ts(sl(Y, 32, 48), ml[0], float(-OFF), -1.0, ALU.add, ALU.max)
+            ts(sl(Y, 48, 64), M3, float(-OFF), -1.0, ALU.add, ALU.max)
+            for i in range(8):
+                y = sl(Y, 8 * i, 8 * i + 8)
+                dma("S", T.ym[:, 128 * i:128 * i + 128], ap(y), [y], [], 4096)
+            xo = sl(xw, OFF, OFF + 1024)
+            dma("S", T.yx[:], ap(xo), [xo], [], 262144)
+            dma("A", T.yz[:], ap(come), [come], [], 24576)
+        else:
+            ts(ml[0], sl(FM, 16, 32), 1.0, None, ALU.min)
+            tt(ml[1], sl(FM, 16, 32), sl(FM, 0, 16), ALU.subtract)
+            tt(ml[0], ml[0], ml[1], ALU.mult)
+            tt(ml[0], ml[0], sl(FM, 0, 16), ALU.add)
+            tt(ml[1], M3, ml[0], ALU.subtract)
+            tt(ml[1], ml[1], hh, ALU.mult)
+            tt(ml[2], ml[1], ml[0], ALU.add)
+            cp(Lml, ml[2])
+            move(g0, (nbw, LI))
+            move(hs, (swpw, LC))
+            tt(sl(gd, 0, 384, 2), sl(g0, 1, 384, 2), sl(g0, 0, 384, 2), ALU.subtract)
+            tt(sl(gd, 0, 384, 2), sl(gd, 0, 384, 2), sl(hs, 0, 384, 2), ALU.mult)
+            times(sl(gd, 1, 384, 2), sl(gd, 0, 384, 2), -1.0)
+            tt((nbw, Lsc), g0, gd, ALU.add)
+            for s in (1, 0):
+                hf = lambda t: half(t, s)
+                xs = sl(xl, 128 * s, 128 * s + 128)
+                move(xs, (xw, hf(Lml)))
+                o = PS(4 + s, 0, 8)
+                a0 = 12 if s == 0 else 0
+                mm([(o, sl(WSEL, 128 * a, 128 * a + 128), sl(xs, a, 128, 16), a == a0, s == 1 and a == 15) for a in range(a0, 16)])
+                if s == 0:
+                    mm([(o, sl(WSEL, 128 * a, 128 * a + 128), sl(come, 8 * a, 8 * a + 8), False, a == 11) for a in range(12)])
+                ts(hf(m0i), o, 37.0, None, ALU.mult)
+                cp(hf(ui), o)
+                ts(hf(ui), hf(ui), 4095, None, ALU.bitwise_and)
+                tt(hf(sq), hf(ui), hf(ui), ALU.mult)
+                tt(hf(m0i), hf(m0i), hf(lanef), ALU.add)
+                ts(hf(sq), hf(sq), 5, 63, ALU.logical_shift_right, ALU.bitwise_and)
+                ts(hf(m0i), hf(m0i), 4095, None, ALU.bitwise_and)
+                tt(hf(Ti), hf(sq), hf(lanef), ALU.add)
+                ts(hf(Ti), hf(Ti), 63, None, ALU.bitwise_and)
+            mi, ti = m0i, Ti
+    LAST["top"] = dict(top)
+    return ops
+
+
+def cyc(c, C):
+    k, n = c
+    if k == "raw":
+        return n
+    if k == "pe":
+        return n * C["pe"]
+    if k == "el":
+        return max(64.0, n) + C["fix"]
+    return 60.0 + n * C[k]
+
+
+def replay(ops, order, eng, C):
+    fin = [0.0] * len(ops)
+    free = {}
+    lat = C["lat"]
+    for i in order:
+        o = ops[i]
+        e = eng[i]
+        t = free.get(e, 0.0)
+        for j in o["deps"]:
+            x = fin[j] + (0.0 if e == "P" and eng[j] == "P" else lat)
+            if x > t:
+                t = x
+        fin[i] = t + cyc(o["cost"][e], C)
+        free[e] = t + (0.0 if e == "X" else cyc(o["hold"][e], C))
+    return max(fin)
+
+
+def place(ops, seq, pred, dur, hold, C, back, fixed):
+    st = [0.0] * len(ops)
+    fin = [0.0] * len(ops)
+    eng = [None] * len(ops)
+    busy = {}
+    lat = C["lat"]
+    for i in seq:
+        best = None
+        isp = "P" in dur[i]
+        t0 = 0.0
+        for j in pred[i]:
+            x = fin[j] + (0.0 if (isp and eng[j] == "P") else lat)
+            if x > t0:
+                t0 = x
+        for e in (dur[i] if fixed is None else (fixed[i],)):
+            h = hold[i][e]
+            sh = dur[i][e] - h if back else 0.0
+            t = t0 + sh
+            S, E = busy.setdefault(e, ([], []))
+            lo, hi = 0, len(E)
+            while lo < hi:
+                m = (lo + hi) // 2
+                if E[m] <= t:
+                    lo = m + 1
+                else:
+                    hi = m
+            while lo < len(S) and S[lo] < t + h:
+                t = max(t, E[lo])
+                lo += 1
+            key = t - sh + dur[i][e] * (1.0 + BETA[0] if e == "V" else 1.0)
+            if best is None or key < best[0]:
+                best = (key, e, t, lo, h, sh)
+        f, e, t, k, h, sh = best
+        if h > 0:
+            busy[e][0].insert(k, t)
+            busy[e][1].insert(k, t + h)
+        st[i] = t - sh
+        fin[i] = t - sh + dur[i][e]
+        eng[i] = e
+    return st, fin, eng
+
+
+def topo_order(ops, succ, pr):
+    left = [len(o["deps"]) for o in ops]
+    idx = sorted(range(len(ops)), key=lambda i: (-pr[i], i))
+    out = []
+    late = set()
+    for i in idx:
+        if left[i] > 0:
+            late.add(i)
+            continue
+        stack = [i]
+        while stack:
+            a = stack.pop()
+            out.append(a)
+            for k in succ[a]:
+                left[k] -= 1
+                if left[k] == 0 and k in late:
+                    late.discard(k)
+                    stack.append(k)
+    return out
+
+
+def optimise(ops, C, lead, steps):
+    n = len(ops)
+    dur = [{e: cyc(c, C) for e, c in o["cost"].items()} for o in ops]
+    hold = [{e: (0.0 if e == "X" else cyc(c, C)) for e, c in o["hold"].items()} for o in ops]
+    pred = [o["deps"] for o in ops]
+    succ = [[] for _ in range(n)]
+    for i in range(n):
+        for j in pred[i]:
+            succ[j].append(i)
+    pr = [0.0] * n
+    for i in range(n - 1, -1, -1):
+        pr[i] = min(dur[i].values()) + max([pr[k] + C["lat"] for k in succ[i]] + [0.0])
+    pr = [pr[i] + (lead if ops[i]["tag"] == 1 else 0.0) for i in range(n)]
+
+    def make(p):
+        st, fin, eng = place(ops, topo_order(ops, succ, p), pred, dur, hold, C, False, None)
+        st, fin, e2 = place(ops, sorted(range(n), key=lambda i: (-fin[i], -i)), succ, dur, hold, C, True, eng)
+        st, fin, eng = place(ops, sorted(range(n), key=lambda i: (-fin[i], i)), pred, dur, hold, C, False, None)
+        order = sorted(range(n), key=lambda i: (st[i], i))
+        return (sum(replay(ops, order, eng, c) for c in RANGE) / len(RANGE), order, eng, st)
+
+    best = make(pr)
+    rs = np.random.RandomState(1)
+    for it in range(steps):
+        st = np.array(best[3])
+        near = np.abs(st - rs.rand() * st.max()) < [4000.0, 10000.0][it % 2]
+        p = -st + near * rs.randn(n) * [100.0, 300.0, 800.0][it % 3]
+        x = make([float(v) for v in p])
+        if x[0] < best[0]:
+            best = x
+    return best
+
+
+def choose(T, rank, core, topo):
+    ops = build(T, rank, core, topo, PLAN)
+    lead = min(LEADS, key=lambda v: optimise(ops, COST, v, 0)[0])
+    return optimise(ops, COST, lead, STEPS)
+
+
+def rank_program(g, core, T, topo):
+    rank = T.rank_of(core)
+    if rank is None:
+        return
+    if "best" not in LAST:
+        LAST["best"] = choose(T, rank, core, topo)
+    order, eng = list(LAST["best"][1]), LAST["best"][2]
+    ops = build(T, rank, core, topo, PLAN)
+    for i, o in enumerate(ops):
+        o["eng"] = eng[i]
+    first = [k for k, i in enumerate(order) if ops[i]["kind"] == "d" and not ops[i]["deps"]]
+    head = sorted(order[k] for k in first)
+    order = head + [i for i in order if i not in head]
+    Q = {"V": g.vector, "A": g.scalar, "P": g.tensor, "G": g, "S": g.sync}
+    pos = {}
+    for k, i in enumerate(order):
+        pos[i] = k
+    need = {}
+    marked = set()
+    seen = {}
+    for i in order:
+        o = ops[i]
+        if o["kind"] == "x":
+            continue
+        lat = {}
+        other = []
+        for j in o["deps"]:
+            p = ops[j]
+            if p["kind"] == "c":
+                if p["eng"] == "P" and o["eng"] == "P":
+                    continue
+                if p["eng"] not in lat or pos[j] > pos[lat[p["eng"]]]:
+                    lat[p["eng"]] = j
+            else:
+                other.append(j)
+        w = []
+        for e, j in lat.items():
+            if seen.get((o["eng"], e), -1) < pos[j]:
+                seen[(o["eng"], e)] = pos[j]
+                marked.add(j)
+                w.append(j)
+        for j in other:
+            if (o["eng"], j) not in seen:
+                seen[(o["eng"], j)] = 1
+                w.append(j)
+        need[i] = w
+    count = {}
+    value = {}
+    for i in order:
+        o = ops[i]
+        if o["kind"] == "c" and i in marked:
+            count[o["eng"]] = count.get(o["eng"], 0) + 1
+            value[i] = ("c" + o["eng"], count[o["eng"]])
+        elif o["kind"] == "d":
+            value[i] = (o["sem"], 16)
+        elif o["kind"] in ("r", "x"):
+            value[i] = o["sem"]
+    waited = set()
+    for i in order:
+        o = ops[i]
+        if o["kind"] == "x":
+            continue
+        q = Q[o["eng"]]
+        for j in need[i]:
+            q.wait_ge(T.sem[value[j][0]], value[j][1])
+            waited.add(j)
+        ins = o["fn"][o["eng"]](q)
+        if o["kind"] == "d":
+            ins.then_inc(T.sem[o["sem"]], 16)
+        elif o["kind"] == "c" and i in marked:
+            ins.then_inc(T.sem[value[i][0]], 1)
+    for i in order:
+        if ops[i]["kind"] != "c" and i not in waited:
+            g.sync.wait_ge(T.sem[value[i][0]], value[i][1])

@@ -11,7 +11,7 @@ SCRATCH = {
     "xw": ("sbuf", [128, NW], "bfloat16"),
     "iow": ("sbuf", [128, NW], "float32"),
     "sf": ("sbuf", [128, 14336], "float32"),
-    "sb": ("sbuf", [128, 36864], "bfloat16"),
+    "sb": ("sbuf", [128, 37888], "bfloat16"),
     "sh": ("sbuf", [128, 4096], "float16"),
     "su": ("sbuf", [128, 2048], "uint16"),
     "si": ("sbuf", [128, 1024], "int32"),
@@ -23,12 +23,13 @@ for _k in range(8):
 NDMA = 40
 SEMAPHORES = ["cV", "cA", "cP", "cG", "arr0", "arr1", "loc0", "loc1"] + ["d%d" % _k for _k in range(NDMA)]
 
-COST = {"ga": 1.56, "sc": 3.8, "pe": 0.5, "lat": 100.0, "fix": 10.0}
-RANGE = [dict(COST, ga=1.15, sc=2.2), COST, dict(COST, ga=1.95, sc=5.4)]
-PLAN = ["FMMM", "MMMM"]
-LEADS = [2500.0, 3000.0, 3500.0, 4000.0]
-STEPS = 500
-BETA = [0.5]
+COST = {"ga": 1.56, "sc": 3.8, "pe": 0.65, "lat": 250.0, "fix": 0.0}
+RANGE = [dict(COST, lat=300.0, pe=0.5), dict(COST, lat=200.0, pe=0.72, fix=20.0), dict(COST, lat=100.0, pe=0.86),
+         dict(COST, lat=100.0, pe=0.5, fix=10.0)]
+PLAN = ["FFMM", "FMMM"]
+LEADS = [3000.0, 4000.0, 5000.0, 6000.0]
+STEPS = 450
+BETA = [1.0]
 LAST = {}
 
 
@@ -357,15 +358,16 @@ def build(T, rank, core, topo, XENG):
     codg = B(256)
     st = []
     for s in range(2):
-        Z = F(320)
+        Z = F(352)
         ms(Z, 0.0)
         d = {"cu": U(128), "ch": H(128), "ft": [(B(128), B(128), B(128)) for _ in range(4)],
              "eq": [B(128), B(128), B(128)], "xg": B(2048), "D": B(2048), "sg": B(128), "W": F(512),
              "NS": [F(512), F(384), F(256), F(128), F(128)], "S": [sl(Z, 0, 56), sl(Z, 64, 120), sl(Z, 128, 184)],
-             "dl": F(48), "G": F(48), "tm": F(48), "Gz": [sl(Z, 192, 240), sl(Z, 256, 304)], "L": [F(24), F(24), F(24), F(24)],
-             "LPQ": U(24), "LM1": U(8), "dif": F(24), "Bq": F(16), "B1": F(8), "t": [F(8) for _ in range(8)], "g4": F(8)}
+             "dl": F(48), "G": F(48), "tm": F(48), "Gz": [sl(Z, 192, 240), sl(Z, 256, 304)], "L": [F(24), F(24), F(24)],
+             "LPQ": U(24), "LM1": U(8), "dif": F(24), "Bq": F(16), "B1": F(8), "t": [F(8) for _ in range(8)], "g4": F(8),
+             "H0": sl(Z, 320, 344), "H1": F(24), "H2": F(24), "k": [F(8) for _ in range(6)]}
         if nf[s] > 0:
-            d["Fz"], d["Fb"] = B(512 * nf[s]), B(1024)
+            d["Fz"], d["Fb"] = B(512 * nf[s]), B(512 * min(nf[s], 2))
             ms(d["Fz"], 0.0)
         st.append(d)
     Rr, Gw, Gh = F(256), F(768), H(96)
@@ -448,9 +450,9 @@ def build(T, rank, core, topo, XENG):
         d = st[s]
         hf = lambda t: half(t, s)
         fld = lambda S, k: sl(S, k, 48, 6)
-        t = d["t"]
+        tri = lambda X, i: sl(X, i, 24, 3)
+        t, kk, L = d["t"], d["k"], d["L"]
         LP, LQ, LM2 = sl(d["LPQ"], 0, 8), sl(d["LPQ"], 8, 16), sl(d["LPQ"], 16, 24)
-        L = d["L"]
 
         def prep(S, both):
             tt(t[0], hf(w31), fld(S, 2), ALU.mult)
@@ -460,20 +462,41 @@ def build(T, rank, core, topo, XENG):
                 tt(fld(S, 1), t[1], hf(U2), ALU.min)
             tt(d["dl"], sl(S, 0, 48), sl(S, 1, 49), ALU.subtract)
 
+        def parent(N0):
+            cp(tri(d["H0"], 1), N0)
+            ts(tri(d["H0"], 2), N0, 1.0, None, ALU.min)
+            scan(d["H2"], d["H0"], d["H1"], 0.0, ALU.mult, ALU.add)
+            cp(LP, tri(d["H2"], 2))
+
+        def coeff(S, is3, M2, B1, both):
+            K2, K1, K0 = tri(d["H1"], 0), tri(d["H1"], 1), tri(d["H1"], 2)
+            tt(kk[0], hf(w32), is3, ALU.mult)
+            tt(K2, hf(w32), kk[0], ALU.subtract)
+            tt(kk[1], hf(w32), B1, ALU.mult)
+            tt(kk[2], hf(w32), M2, ALU.mult)
+            if both:
+                ts(kk[3], B1, 1.0, None, ALU.min)
+                tt(kk[3], kk[3], fld(d["dl"], 0), ALU.mult)
+                tt(kk[4], kk[1], fld(S, 1), ALU.add)
+                tt(K0, kk[3], kk[4], ALU.add)
+                tt(kk[5], kk[2], fld(S, 0), ALU.add)
+                tt(K1, kk[5], K0, ALU.subtract)
+            else:
+                tt(K0, kk[1], fld(S, 0), ALU.add)
+                tt(K1, kk[2], kk[1], ALU.subtract)
+
         def trans(S, S2, Gz, Bh, Lx, both):
             ts(fld(Gz, 0), Bh, 1.0, None, ALU.min)
-            tt(t[2], hf(w32), Bh, ALU.mult)
             tt(t[3], hf(Q2e), Bh, ALU.max)
             scan(d["G"], SEG6, Gz, 0.0, ALU.mult, ALU.add)
             tt(sl(Lx, 8, 16), t[3], hf(Q3e), ALU.min)
             tt(d["tm"], d["G"], d["dl"], ALU.mult)
             tt(sl(S2, 0, 48), d["tm"], sl(S, 1, 49), ALU.add)
-            tt(sl(Lx, 0, 8), t[2], fld(S2, 0), ALU.add)
             if both:
-                cp(sl(d["LPQ"], 0, 16), sl(Lx, 0, 16))
+                cp(LQ, sl(Lx, 8, 16))
                 cp(LM2, Bh)
             else:
-                cp(d["LPQ"], Lx)
+                cp(sl(d["LPQ"], 8, 24), sl(Lx, 8, 24))
             cp(d["LM1"], fld(S2, 2))
             prep(S2, both)
 
@@ -498,12 +521,18 @@ def build(T, rank, core, topo, XENG):
         for r in range(3):
             relu(fld(S[0], 3 + r), sl(d["dif"], 8 * r, 8 * r + 8))
         prep(S[0], True)
+        move(tri(d["H1"], 0), hf(w32))
+        move(tri(d["H1"], 1), fld(d["dl"], 0))
+        move(tri(d["H1"], 2), fld(S[0], 1))
         N0 = evaluate(s, 1, LP, None, [hf(LM0), d["LM1"]])
+        parent(N0)
         trans(S[0], S[1], d["Gz"][0], N0, L[1], True)
         relu(d["Bq"], sl(d["dif"], 0, 16))
         M2 = N0
-        N0 = evaluate(s, 2, LP, LQ, [hf(LM0), d["LM1"], LM2])
         is3 = fld(d["Gz"][0], 0)
+        coeff(S[1], is3, M2, sl(d["Bq"], 0, 8), True)
+        N0 = evaluate(s, 2, LP, LQ, [hf(LM0), d["LM1"], LM2])
+        parent(N0)
         B3 = sl(L[2], 16, 24)
         mixed(N0, is3, M2, sl(d["Bq"], 0, 8), B3)
         trans(S[1], S[2], d["Gz"][1], B3, L[2], False)
@@ -511,12 +540,11 @@ def build(T, rank, core, topo, XENG):
         tt(t[6], t[5], is3, ALU.mult)
         tt(t[5], t[5], sl(d["Bq"], 8, 16), ALU.add)
         tt(d["B1"], t[5], t[6], ALU.subtract)
+        coeff(S[2], fld(d["Gz"][1], 0), B3, d["B1"], False)
         N0 = evaluate(s, 3, LP, LQ, [hf(LM0), d["LM1"], LM2])
+        parent(N0)
         Bh = hf(sl(FM, 32, 48))
         mixed(N0, fld(d["Gz"][1], 0), B3, d["B1"], Bh)
-        tt(t[2], hf(w32), Bh, ALU.mult)
-        tt(sl(L[3], 0, 8), t[2], fld(S[2], 0), ALU.add)
-        cp(LP, sl(L[3], 0, 8))
         cp(LM2, Bh)
         ts(d["g4"], Bh, 1.0, None, ALU.min)
         tt(t[3], d["g4"], fld(d["dl"], 2), ALU.mult)
@@ -638,7 +666,8 @@ def build(T, rank, core, topo, XENG):
         cp((xw, Lsc), new)
         move(come, (land, Lin))
         if last:
-            ts(sl(Y, 0, 32), sl(FM, 0, 32), float(-OFF), -1.0, ALU.add, ALU.max)
+            ts(sl(Y, 0, 16), sl(FM, 0, 16), float(-OFF), -1.0, ALU.add, ALU.max)
+            ts(sl(Y, 16, 32), sl(FM, 16, 32), float(-OFF), -1.0, ALU.add, ALU.max)
             tt(ml[0], sl(FM, 32, 48), hh, ALU.mult)
             ts(sl(Y, 32, 48), ml[0], float(-OFF), -1.0, ALU.add, ALU.max)
             ts(sl(Y, 48, 64), M3, float(-OFF), -1.0, ALU.add, ALU.max)
@@ -826,8 +855,7 @@ def rank_program(g, core, T, topo):
     ops = build(T, rank, core, topo, PLAN)
     for i, o in enumerate(ops):
         o["eng"] = eng[i]
-    first = [k for k, i in enumerate(order) if ops[i]["kind"] == "d" and not ops[i]["deps"]]
-    head = sorted(order[k] for k in first)
+    head = sorted(i for i in order if ops[i]["kind"] == "d" and not ops[i]["deps"])
     order = head + [i for i in order if i not in head]
     Q = {"V": g.vector, "A": g.scalar, "P": g.tensor, "G": g, "S": g.sync}
     pos = {}

import numpy as np
from concourse.bass import DstId, RemoteDMATransfer
from concourse.mybir import AluOpType as ALU, ActivationFunctionType as ACT

OFF = 512
MID = OFF + 2048
NW = 4096 + OFF
SCRATCH = {
    "nbi": ("sbuf", [128, 4096], "int32"),
    "nbw": ("sbuf", [128, NW], "float32"),
    "xw": ("sbuf", [128, NW], "bfloat16"),
    "iow": ("sbuf", [128, NW], "float32"),
    "sf": ("sbuf", [128, 14336], "float32"),
    "sb": ("sbuf", [128, 37888], "bfloat16"),
    "sh": ("sbuf", [128, 4096], "float16"),
    "su": ("sbuf", [128, 2048], "uint16"),
    "si": ("sbuf", [128, 1024], "int32"),
    "land0": ("sbuf", [128, 112], "bfloat16"),
    "land1": ("sbuf", [128, 112], "bfloat16"),
}
for _k in range(8):
    SCRATCH["ps%d" % _k] = ("psum", [128, 512], "float32")
NDMA = 40
SEMAPHORES = ["cV", "cA", "cP", "cG", "arr0", "arr1", "loc0", "loc1"] + ["d%d" % _k for _k in range(NDMA)]

COST = {"ga": 1.56, "sc": 3.8, "pe": 0.65, "lat": 250.0, "fix": 0.0}
RANGE = [dict(COST, lat=300.0, pe=0.5), dict(COST, lat=200.0, pe=0.72, fix=20.0), dict(COST, lat=100.0, pe=0.86),
         dict(COST, lat=100.0, pe=0.5, fix=10.0)]
PLAN = ["FFMM", "FMMM"]
LEADS = [3000.0, 4000.0, 5000.0, 6000.0]
STEPS = 450
BETA = [1.0]
LAST = {}


def build(T, rank, core, topo, XENG):
    ops = []
    hist = {}
    tag = [None]
    top = {"sf": 0, "sb": 0, "sh": 0, "su": 0, "si": 0}
    size = {"sf": 4, "sb": 2, "sh": 2, "su": 2, "si": 4, "nbi": 4, "nbw": 4, "xw": 2, "iow": 4, "land0": 2, "land1": 2}

    def al(buf, n):
        a = top[buf]
        top[buf] = a + (n + 15) // 16 * 16
        return (buf, a, a + n, 1)

    def sl(t, a, b, s=1):
        n = (b - a + s - 1) // s
        lo = t[1] + a * t[3]
        return (t[0], lo, lo + (n - 1) * s * t[3] + 1, s * t[3])

    def cnt(t):
        return (t[2] - t[1] + t[3] - 1) // t[3]

    def ap(t):
        if len(t) == 2:
            return ap(t[0]).indirect(ap(t[1]))
        if t[3] == 1:
            return T[t[0]][:, t[1]:t[2]]
        return T[t[0]][:, t[1]:t[2]:t[3]]

    def isps(t):
        return t[0][:2] == "ps"

    def tiles(xs):
        r = []
        for x in xs:
            if isinstance(x, tuple):
                if len(x) == 2:
                    r += [x[0], x[1]]
                else:
                    r.append(x)
        return r

    def val(x):
        return ap(x) if isinstance(x, tuple) else x

    def add(eng, fn, reads, writes, cost, kind="c", hold=None, extra=(), sem=None):
        i = len(ops)
        deps = set(extra)
        acc = [(t, False) for t in reads] + [(t, True) for t in writes]
        for t, w in acc:
            lo, hi = (0, 512) if isps(t) else (t[1], t[2])
            w = w or isps(t)
            for (j, l2, h2, w2, s2) in hist.get(t[0], []):
                if (w or w2) and l2 < hi and lo < h2 and (isps(t) or s2 != t[3] or (lo - l2) % s2 == 0):
                    deps.add(j)
        for t, w in acc:
            lo, hi = (0, 512) if isps(t) else (t[1], t[2])
            w = w or isps(t)
            h = hist.setdefault(t[0], [])
            if w and (isps(t) or t[3] == 1):
                h[:] = [e for e in h if not (lo <= e[1] and e[2] <= hi)]
            h.append((i, lo, hi, w, t[3]))
        deps.discard(i)
        ops.append({"fn": {eng: fn}, "deps": sorted(deps), "cost": {eng: cost}, "kind": kind,
                    "hold": {eng: cost if hold is None else hold}, "sem": sem, "tag": tag[0]})
        return i

    def vcost(out, ins, two=False):
        if len(out) == 2:
            return ("sc", 16 * cnt(out[1]))
        for x in ins:
            if isinstance(x, tuple) and len(x) == 2:
                return ("ga", 16 * cnt(x[1]))
        n = cnt(out)
        ts_ = tiles([out] + ins)
        if two:
            return ("el", n * (1.0 if any(isps(t) for t in ts_[1:]) else 2.0))
        return ("el", n * (0.5 if all((not isps(t)) and size[t[0]] == 2 for t in ts_) else 1.0))

    def wr(out):
        return ([out[1]], [out[0]]) if len(out) == 2 else ([], [out])

    def tt(out, a, b, op):
        r, w = wr(out)
        return add("V", lambda q: q.tensor_tensor(ap(out), ap(a), ap(b), op), tiles([a, b]) + r, w, vcost(out, [a, b], True))

    def ts(out, a, s1, s2, op0, op1=None):
        r, w = wr(out)
        if op1 is None:
            f = lambda q: q.tensor_scalar(ap(out), ap(a), val(s1), None, op0)
        else:
            f = lambda q: q.tensor_scalar(ap(out), ap(a), val(s1), val(s2), op0, op1)
        return add("V", f, tiles([a, s1, s2]) + r, w, vcost(out, [a]))

    def cp(out, a):
        r, w = wr(out)
        return add("V", lambda q: q.tensor_copy(ap(out), ap(a)), tiles([a]) + r, w, vcost(out, [a]))

    def ms(out, c):
        return add("V", lambda q: q.memset(ap(out), c), [], [out], vcost(out, []))

    def scan(out, d0, d1, init, op0, op1):
        return add("V", lambda q: q.tensor_tensor_scan(ap(out), ap(d0), ap(d1), val(init), op0, op1),
                   tiles([d0, d1, init]), [out], vcost(out, [d0, d1]))

    def act(out, a, func, bias=None, scale=None):
        kw = {}
        if bias is not None:
            kw["bias"] = val(bias)
        if scale is not None:
            kw["scale"] = val(scale)
        c = ("ga", 16 * cnt(a[1])) if len(a) == 2 else ("el", float(cnt(out)))
        return add("A", lambda q: q.activation(ap(out), ap(a), func, **kw), tiles([a, bias, scale]), [out], c)

    def either(i, out, a, f):
        ops[i]["fn"]["V"] = f
        ops[i]["cost"]["V"] = vcost(out, [a])
        ops[i]["hold"]["V"] = vcost(out, [a])

    def move(out, a):
        either(act(out, a, ACT.Copy), out, a, lambda q: q.tensor_copy(ap(out), ap(a)))

    def relu(out, a, b=0.0):
        either(act(out, a, ACT.Relu, bias=b), out, a, lambda q: q.tensor_scalar(ap(out), ap(a), val(b), 0.0, ALU.add, ALU.max))

    def times(out, a, c):
        either(act(out, a, ACT.Identity, scale=c), out, a, lambda q: q.tensor_scalar(ap(out), ap(a), val(c), None, ALU.mult))

    def plus(out, a, c):
        either(act(out, a, ACT.Identity, bias=c), out, a, lambda q: q.tensor_scalar(ap(out), ap(a), val(c), None, ALU.add))

    def mm(lst):
        def f(q):
            r = None
            for (o, l, rr, st, sp) in lst:
                r = q.matmul(ap(o), ap(l), ap(rr), st, sp)
            return r
        c = sum(max(64, cnt(rr)) * (4 if size[rr[0]] == 4 else 1) for (o, l, rr, st, sp) in lst)
        return add("P", f, tiles([x for m in lst for x in m[1:3]]), [m[0] for m in lst], ("pe", c))

    def iota(out, pat, base, cm, flag=True):
        if flag:
            f = lambda q: q.iota(ap(out), pat, base, cm, allow_small_or_imprecise_dtypes=True)
        else:
            f = lambda q: q.iota(ap(out), pat, base, cm)
        return add("G", f, [], [out], ("raw", 160 + 2 * cnt(out)))

    def asel(out, a, pat, op, fill, base, cm):
        return add("G", lambda q: q.affine_select(ap(out), ap(a), pat, op, fill, base, cm), [a], [out], ("raw", 200 + 2 * cnt(out)))

    nd = [0]

    def dma(eng, oap, iap, reads, writes, nbytes):
        s = "d%d" % nd[0]
        nd[0] += 1
        return add(eng, lambda q: q.dma_start(oap, iap), reads, writes, ("raw", 2400 + nbytes / 200.0), kind="d", hold=("raw", 80), sem=s)

    F = lambda n: al("sf", n)
    B = lambda n: al("sb", n)
    U = lambda n: al("su", n)
    I = lambda n: al("si", n)
    H = lambda n: al("sh", n)
    PS = lambda k, a, b: ("ps%d" % k, a, b, 1)
    half = lambda t, s: sl(t, 8 * s, 8 * s + 8)
    nbw = ("nbw", 0, NW, 1)
    xw = ("xw", 0, NW, 1)
    iow = ("iow", 0, NW, 1)

    begi, taui = I(16), I(16)
    parA, parB, wti = I(64), I(64), I(16)
    featw, chgw, swpw = B(208), B(256), B(256)
    ms(parB, 0)
    tload = 0
    for c in range(4):
        t = ("nbi", 1024 * c, 1024 * c + 1024, 1)
        tload += 524288
        dma("S", ap(t), T.nb[:, 1024 * c:1024 * c + 1024], [], [t], tload)
        ts(sl(nbw, OFF + 1024 * c, OFF + 1024 * c + 1024), t, float(OFF), None, ALU.add)
    for c in range(2):
        t = sl(xw, OFF + 2048 * c, OFF + 2048 * c + 2048)
        tload += 524288
        dma("S", ap(t), T.x[:, 2048 * c:2048 * c + 2048], [], [t], tload)
    for s in (1, 0):
        dma("A", ap(half(taui, s)), T.tau[:, 128 * s:128 * s + 128], [], [half(taui, s)], 4096)
        dma("A", ap(half(begi, s)), T.beg[:, 128 * s:128 * s + 128], [], [half(begi, s)], 4096)
    dma("A", ap(parA), T.par[:], [], [parA], 32768)
    dma("A", ap(sl(featw, 16, 208)), T.feat[:], [], [sl(featw, 16, 208)], 49152)
    dma("A", T.si[0:125, parB[1]:parB[2]], T.par[3:128, :], [], [parB], 32768)
    dma("S", ap(chgw), T.chg[:], [], [chgw], tload)
    dma("S", ap(sl(swpw, 0, 64)), T.swp[:], [], [sl(swpw, 0, 64)], tload)
    dma("S", ap(sl(wti, 0, 1)), T.wt[:], [], [wti], tload)
    ms(sl(nbw, 0, OFF), 16.0)
    ms(sl(xw, 0, OFF), 0.0)
    ms(sl(xw, 16, 32), 8192.0)
    ms(sl(featw, 0, 16), 0.0)

    pi_, pki, tmpi = I(1), I(1), I(8)
    pk = F(1)
    iota(pi_, [[0, 1]], 0, 1, False)
    ts(pki, pi_, 15, None, ALU.bitwise_and)
    cp(pk, pki)
    iota(sl(iow, 0, 512), [[1, 512]], -MID, 0)
    for c in range(1, NW // 512):
        plus(sl(iow, 512 * c, 512 * c + 512), sl(iow, 0, 512), float(512 * c))
    BOf, ONE, IDf, ONEb = F(128), F(512), F(128), B(512)
    ms(ONE, 1.0)
    ms(ONEb, 1.0)
    inblock = lambda o, a, n, fill: (asel(o, a, [[0, n], [-16, 8], [0, 16]], ALU.is_ge, fill, 0, 1),
                                     asel(o, o, [[0, n], [16, 8], [0, 16]], ALU.is_ge, fill, 15, -1))
    inblock(BOf, sl(ONE, 0, 128), 1, 0.0)
    asel(IDf, sl(ONE, 0, 128), [[-1, 128]], ALU.is_equal, 0.0, 0, 1)
    BO, NBO, ID, BIGI, N128I, TRI, TRI1 = B(128), B(128), B(128), B(128), B(128), B(128), B(128)
    IDh = H(128)
    move(BO, BOf)
    times(NBO, BOf, -1.0)
    move(ID, IDf)
    cp(IDh, IDf)
    times(BIGI, IDf, 8192.0)
    times(N128I, IDf, -128.0)
    asel(TRI1, BO, [[1, 128]], ALU.is_gt, 0.0, 0, -1)
    trf = F(128)
    times(trf, IDf, -8.0)
    tt(trf, trf, TRI1, ALU.add)
    times(TRI, trf, 4096.0)
    SELN, SEL, WSEL = B(2048), B(2048), B(2048)
    ms(SELN, -1.0)
    asel(SELN, SELN, [[1, 128], [0, 16]], ALU.is_equal, 0.0, 0, -1)
    io16, DEL, iob = F(128), F(128), B(128)
    iota(io16, [[0, 8], [1, 16]], 0, 0)
    iota(iob, [[0, 8], [1, 16]], 0, 0)
    inblock(iob, iob, 1, -1.0)
    for k in range(16):
        ts(sl(SEL, 128 * k, 128 * k + 128), iob, float(k), None, ALU.is_equal)
    SELf, SELh = F(128), H(640)
    move(SELf, sl(SEL, 384, 512))
    cp(SELh, sl(SEL, 0, 640))
    wtf = F(1)
    cp(wtf, sl(wti, 0, 1))
    for k in range(4):
        times(sl(WSEL, 512 * k, 512 * k + 512), sl(SEL, 512 * k, 512 * k + 512), wtf)
    ts(DEL, io16, pk, None, ALU.is_equal)
    dcol = lambda k: sl(DEL, k, k + 1)
    DM = B(512)
    for r in range(4):
        ts(sl(DM, 128 * r, 128 * r + 128), DEL, float(2 ** 20 - 4096 * r * (r + 1)), float(-2 ** 20), ALU.mult, ALU.add)
    SEGM, SEG6, SEG8, SEG4f, SEG4, SEGb = F(384), F(48), F(16), F(384), B(384), B(512)
    asel(SEGM, sl(ONE, 0, 384), [[0, 24], [1, 16]], ALU.is_gt, 0.0, 0, 0)
    asel(SEG6, sl(ONE, 0, 48), [[0, 8], [1, 6]], ALU.is_gt, 0.0, 0, 0)
    asel(SEG8, sl(ONE, 0, 16), [[0, 2], [1, 8]], ALU.is_gt, 0.0, 0, 0)
    asel(SEG4f, sl(ONE, 0, 384), [[0, 96], [1, 4]], ALU.is_gt, 0.0, 0, 0)
    asel(SEG4, sl(ONEb, 0, 384), [[0, 96], [1, 4]], ALU.is_gt, 0.0, 0, 0)
    nf = [XENG[0].count("F"), XENG[1].count("F")]
    if nf[0] + nf[1] > 0:
        asel(SEGb, ONEb, [[0, 32], [1, 16]], ALU.is_gt, 0.0, 0, 0)
    WB = F(4)
    for r in range(4):
        ts(sl(WB, r, r + 1), pk, -4096.0, float(MID - 32768 + 8192 * r), ALU.mult, ALU.add)
    thrw, codw = B(208), B(80)
    hiA, loB = I(64), I(64)
    ta, tb, ccol = F(64), F(64), F(1)
    ms(sl(thrw, 0, 16), -1.0)
    ms(sl(codw, 0, 16), 0.0)
    ts(hiA, parA, 4080, None, ALU.bitwise_and)
    ts(loB, parB, 15, None, ALU.bitwise_and)
    for j in range(1, 4):
        ts(ta, hiA, dcol(8 + j), None, ALU.mult)
        ts(tb, loB, dcol(5 + j), None, ALU.mult)
        tt(sl(thrw, 16 + 64 * (j - 1), 16 + 64 * j), ta, tb, ALU.add)
    ts(ccol, dcol(3), 2.0, dcol(2), ALU.mult, ALU.add)
    ts(sl(codw, 16, 80), parA, ccol, None, ALU.mult)
    move(sl(swpw, 64, 128), sl(swpw, 0, 64))
    move(sl(swpw, 128, 256), sl(swpw, 0, 128))
    AQ, AT, AQh, ATh, RSh, gofs = F(512), F(512), H(512), H(512), H(512), F(1)
    asel(AQ, ONE, [[4, 4], [-16, 8], [-1, 16]], ALU.is_equal, 0.0, 0, 1)
    asel(AQ, AQ, [[0, 4], [-16, 8], [0, 16]], ALU.is_ge, 0.0, 0, 1)
    asel(AQ, AQ, [[0, 4], [16, 8], [0, 16]], ALU.is_ge, 0.0, 3, -1)
    asel(AT, ONE, [[0, 4], [-16, 8], [0, 16]], ALU.is_equal, 0.0, -4, 1)
    asel(AT, AT, [[-4, 4], [0, 8], [1, 16]], ALU.is_ge, 0.0, 0, 0)
    asel(AT, AT, [[4, 4], [0, 8], [-1, 16]], ALU.is_ge, 0.0, 3, 0)
    cp(AQh, AQ)
    cp(ATh, AT)
    for i in range(4):
        ts(sl(RSh, 128 * i, 128 * i + 128), BOf, dcol(i), None, ALU.mult)
    ts(gofs, dcol(4), float(MID), float(-MID), ALU.mult, ALU.add)
    c64, rofs = F(1), F(1)
    ts(rofs, dcol(3), float(-MID), None, ALU.mult)
    ts(sl(tmpi, 1, 2), pi_, 3, None, ALU.bitwise_and)
    ts(c64, sl(tmpi, 1, 2), 64.0, None, ALU.mult)
    w0, w1, w2, wcol, thr96, q8, q2, zer = F(1), F(1), F(1), F(24), F(96), F(24), F(96), F(96)
    ts(sl(tmpi, 2, 3), pi_, 2, 1, ALU.logical_shift_right, ALU.bitwise_and)
    ts(sl(tmpi, 3, 4), pi_, 3, 1, ALU.logical_shift_right, ALU.bitwise_and)
    ts(w0, sl(tmpi, 2, 3), -0.75 * 2.0 ** 96, 2.0 ** 96, ALU.mult, ALU.add)
    ts(w1, sl(tmpi, 3, 4), -0.9375, 1.0, ALU.mult, ALU.add)
    tt(w2, w0, w1, ALU.mult)
    ms(q8, 2.0 ** -8)
    ms(q2, 0.25)
    ms(zer, 0.0)
    scan(wcol, q8, sl(zer, 0, 24), w2, ALU.mult, ALU.add)
    scan(thr96, q2, zer, 7.0 * 2.0 ** 90, ALU.mult, ALU.add)
    ioc, iol = F(24), F(16)
    iota(ioc, [[1, 24]], 0, 0)
    iota(iol, [[128, 2], [1, 8]], 0, 0)
    lanef, dum16, neg16, n24, dum24, pk8, pk7 = F(16), F(16), F(16), F(24), F(24), F(1), F(1)
    ts(pk8, pk, 8.0, None, ALU.mult)
    ts(lanef, iol, pk8, None, ALU.add)
    ts(dum16, lanef, 256.0, None, ALU.add)
    ts(neg16, lanef, -1.0, -257.0, ALU.mult, ALU.add)
    ts(n24, ioc, 16.0, pk, ALU.mult, ALU.add)
    ts(dum24, n24, 64.0, None, ALU.add)
    t6, q6, o6, r6 = F(6), I(6), F(6), F(6)
    Lout, Lin = U(8), U(6)
    ts(pk7, pk, 7.0, None, ALU.mult)
    ts(Lout, sl(ioc, 0, 8), pk7, 95.0, ALU.add, ALU.min)
    ts(r6, sl(n24, 0, 6), -3.0, 1.0 / 7.0, ALU.add, ALU.mult)
    cp(q6, r6)
    ts(t6, q6, -111.0, None, ALU.mult)
    ts(o6, sl(n24, 0, 6), 16.0, None, ALU.mult)
    tt(o6, o6, t6, ALU.add)
    cp(Lin, o6)

    FM, M3, Ew = F(64), F(16), H(1024)
    LM0, LQ1, LQ2, LQ3 = U(16), U(16), U(16), U(16)
    Q2e, Q3e, C2, U2, K30, w32 = F(16), F(16), F(16), F(16), F(16), F(16)
    w21, w31, codi = I(16), I(16), I(16)
    codg = B(256)
    st = []
    for s in range(2):
        Z = F(352)
        ms(Z, 0.0)
        d = {"cu": U(128), "ch": H(128), "ft": [(B(128), B(128), B(128)) for _ in range(4)],
             "eq": [B(128), B(128), B(128)], "xg": B(2048), "D": B(2048), "sg": B(128), "W": F(512),
             "NS": [F(512), F(384), F(256), F(128), F(128)], "S": [sl(Z, 0, 56), sl(Z, 64, 120), sl(Z, 128, 184)],
             "dl": F(48), "G": F(48), "tm": F(48), "Gz": [sl(Z, 192, 240), sl(Z, 256, 304)], "L": [F(24), F(24), F(24)],
             "LPQ": U(24), "LM1": U(8), "dif": F(24), "Bq": F(16), "B1": F(8), "t": [F(8) for _ in range(8)], "g4": F(8),
             "H0": sl(Z, 320, 344), "H1": F(24), "H2": F(24), "k": [F(8) for _ in range(6)]}
        if nf[s] > 0:
            d["Fz"], d["Fb"] = B(512 * nf[s]), B(512 * min(nf[s], 2))
            ms(d["Fz"], 0.0)
        st.append(d)
    Rr, Gw, Gh = F(256), F(768), H(96)
    hh, hb, sc_, a1, Y = F(16), F(16), B(16), F(16), F(64)
    Lsl, LI, LC, Lsc, Lml = U(16), U(24), U(24), U(24), U(16)
    If, dI, of = F(24), F(24), F(24)
    rep = U(384)
    eqb = B(4800)
    okh = H(96)
    xc, cc, sgn, new, zm, zz, zs, come, xl = B(384), B(384), B(384), B(384), B(384), B(96), B(128), B(96), B(256)
    g0, gd, hs = F(384), F(384), B(384)
    ui, sq, m0i, Ti = I(16), I(16), I(16), I(16)
    ml = [F(16), F(16), F(16)]

    def feats(s, lq, Fg, FT, Tg):
        ex = 4 + s
        move(Fg, (featw, lq))
        mm([(PS(ex, 0, 128), Fg, ID, True, True)])
        move(FT, PS(ex, 0, 128))
        move(Tg, (thrw, lq))

    def evaluate(s, e, lp, lq, cmps):
        d = st[s]
        R = 4 - e if e < 4 else 1
        sb_, ex = 6 + s, 4 + s
        cp(d["cu"], (nbw, lp))
        ts(d["ch"], d["cu"], float(-MID), None, ALU.add)
        Fg, FT, Tg = d["ft"][[0, 1, 3, 3, 2][e]]
        if lq is not None:
            feats(s, lq, Fg, FT, Tg)
        if nf[s] > 0:
            move(sl(d["Fz"], 0, 512 * nf[s], 16), sl(Fg, 0, 32 * nf[s]))
        for i, lm in enumerate(cmps):
            tt(d["eq"][i], (iow, lm), d["ch"], ALU.is_equal)
        mm([(PS(sb_, 0, 128), NBO, Tg, True, False)])
        for c in range(4):
            xg = sl(d["xg"], 512 * c, 512 * c + 512)
            src = (xw, sl(d["cu"], 32 * c, 32 * c + 32))
            D = sl(d["D"], 512 * c, 512 * c + 512)
            if XENG[s][c] == "F":
                Fb = sl(d["Fb"], 512 * (c % 2), 512 * (c % 2) + 512)
                scan(Fb, SEGb, sl(d["Fz"], 512 * c, 512 * c + 512), 0.0, ALU.mult, ALU.add)
                tt(xg, src, Fb, ALU.subtract)
                act(D, xg, ACT.Abs)
            else:
                bank = PS(2 * s + c % 2, 0, 512)
                move(xg, src)
                mm([(bank, FT, sl(SELN, 512 * c, 512 * c + 512), True, False)])
                mm([(bank, ID, xg, False, True)])
                act(D, bank, ACT.Abs)
            if c % 2 == 1:
                h = c // 2
                if h == 1:
                    mm([(PS(sb_, 0, 128), BIGI, d["eq"][i], False, False) for i in range(len(cmps))])
                mm([(PS(sb_, 64 * h, 64 * h + 64), sl(SEL, 128 * k, 128 * k + 128), sl(d["D"], 1024 * h + k, 1024 * h + 1024, 16),
                     False, h == 1 and k == 15) for k in range(16)])
        act(d["sg"], PS(sb_, 0, 128), ACT.Sign, bias=-0.5)
        X = PS(sb_, 128, 256)
        mm([(X, IDh, d["ch"], True, False), (X, TRI, d["sg"], False, True)])
        NS = d["NS"][e]
        for r in range(R):
            W = sl(d["W"], 128 * r, 128 * r + 128)
            relu(W, X, sl(WB, r, r + 1))
            if r == 0:
                o = PS(ex if e < 4 else 2 * s, 0, 128)
                mm([(o, ID, sl(DM, 0, 128), True, False)])
                mm([(o, BOf, W, False, True)])
                scan(sl(NS, 0, 128), sl(SEGM, 0, 128), o, 0.0, ALU.mult, ALU.max)
        if R > 1:
            o = PS(ex, 128, 512) if e == 0 else PS(sb_, 256, 128 + 128 * R)
            mm([(o, ID, sl(DM, 128, 128 * R), True, False)])
            for r in range(1, R):
                mm([(sl(o, 128 * r - 128, 128 * r), BOf, sl(d["W"], 128 * r, 128 * r + 128), False, r == R - 1)])
            scan(sl(NS, 128, 128 * R), sl(SEGM, 0, 128 * (R - 1)), o, 0.0, ALU.mult, ALU.max)
            V = sl(NS, 15, 128 * R, 16)
            tt(sl(d["dif"], 0, 8 * (R - 1)), sl(V, 8, 8 * R), sl(V, 0, 8 * (R - 1)), ALU.subtract)
        return sl(NS, 15, 128, 16)

    def search(s):
        d = st[s]
        hf = lambda t: half(t, s)
        fld = lambda S, k: sl(S, k, 48, 6)
        tri = lambda X, i: sl(X, i, 24, 3)
        t, kk, L = d["t"], d["k"], d["L"]
        LP, LQ, LM2 = sl(d["LPQ"], 0, 8), sl(d["LPQ"], 8, 16), sl(d["LPQ"], 16, 24)

        def prep(S, both):
            tt(t[0], hf(w31), fld(S, 2), ALU.mult)
            tt(fld(S, 0), t[0], hf(K30), ALU.add)
            if both:
                tt(t[1], hf(C2), fld(S, 3), ALU.mult)
                tt(fld(S, 1), t[1], hf(U2), ALU.min)
            tt(d["dl"], sl(S, 0, 48), sl(S, 1, 49), ALU.subtract)

        def parent(N0):
            cp(tri(d["H0"], 1), N0)
            ts(tri(d["H0"], 2), N0, 1.0, None, ALU.min)
            scan(d["H2"], d["H0"], d["H1"], 0.0, ALU.mult, ALU.add)
            cp(LP, tri(d["H2"], 2))

        def coeff(S, is3, M2, B1, both):
            K2, K1, K0 = tri(d["H1"], 0), tri(d["H1"], 1), tri(d["H1"], 2)
            tt(kk[0], hf(w32), is3, ALU.mult)
            tt(K2, hf(w32), kk[0], ALU.subtract)
            tt(kk[1], hf(w32), B1, ALU.mult)
            tt(kk[2], hf(w32), M2, ALU.mult)
            if both:
                ts(kk[3], B1, 1.0, None, ALU.min)
                tt(kk[3], kk[3], fld(d["dl"], 0), ALU.mult)
                tt(kk[4], kk[1], fld(S, 1), ALU.add)
                tt(K0, kk[3], kk[4], ALU.add)
                tt(kk[5], kk[2], fld(S, 0), ALU.add)
                tt(K1, kk[5], K0, ALU.subtract)
            else:
                tt(K0, kk[1], fld(S, 0), ALU.add)
                tt(K1, kk[2], kk[1], ALU.subtract)

        def trans(S, S2, Gz, Bh, Lx, both):
            ts(fld(Gz, 0), Bh, 1.0, None, ALU.min)
            tt(t[3], hf(Q2e), Bh, ALU.max)
            scan(d["G"], SEG6, Gz, 0.0, ALU.mult, ALU.add)
            tt(sl(Lx, 8, 16), t[3], hf(Q3e), ALU.min)
            tt(d["tm"], d["G"], d["dl"], ALU.mult)
            tt(sl(S2, 0, 48), d["tm"], sl(S, 1, 49), ALU.add)
            if both:
                cp(LQ, sl(Lx, 8, 16))
                cp(LM2, Bh)
            else:
                cp(sl(d["LPQ"], 8, 24), sl(Lx, 8, 24))
            cp(d["LM1"], fld(S2, 2))
            prep(S2, both)

        def mixed(N0, is3, M2, B1, Bh):
            tt(t[5], M2, B1, ALU.subtract)
            tt(t[6], is3, N0, ALU.mult)
            tt(t[0], N0, B1, ALU.add)
            ts(t[7], t[6], 1.0, None, ALU.min)
            tt(t[1], t[0], t[6], ALU.subtract)
            tt(t[7], t[7], t[5], ALU.mult)
            tt(Bh, t[1], t[7], ALU.add)

        S = d["S"]
        for k, lq in enumerate((LQ1, LQ2, LQ3)):
            feats(s, hf(lq), d["ft"][k][0], d["ft"][k][1], d["ft"][k][2])
        N0 = evaluate(s, 0, hf(LM0), None, [hf(LM0)])
        tt(t[2], hf(C2), N0, ALU.mult)
        tt(sl(L[0], 0, 8), t[2], hf(U2), ALU.min)
        cp(LP, sl(L[0], 0, 8))
        cp(d["LM1"], N0)
        move(fld(S[0], 2), N0)
        for r in range(3):
            relu(fld(S[0], 3 + r), sl(d["dif"], 8 * r, 8 * r + 8))
        prep(S[0], True)
        move(tri(d["H1"], 0), hf(w32))
        move(tri(d["H1"], 1), fld(d["dl"], 0))
        move(tri(d["H1"], 2), fld(S[0], 1))
        N0 = evaluate(s, 1, LP, None, [hf(LM0), d["LM1"]])
        parent(N0)
        trans(S[0], S[1], d["Gz"][0], N0, L[1], True)
        relu(d["Bq"], sl(d["dif"], 0, 16))
        M2 = N0
        is3 = fld(d["Gz"][0], 0)
        coeff(S[1], is3, M2, sl(d["Bq"], 0, 8), True)
        N0 = evaluate(s, 2, LP, LQ, [hf(LM0), d["LM1"], LM2])
        parent(N0)
        B3 = sl(L[2], 16, 24)
        mixed(N0, is3, M2, sl(d["Bq"], 0, 8), B3)
        trans(S[1], S[2], d["Gz"][1], B3, L[2], False)
        relu(t[5], sl(d["dif"], 0, 8))
        tt(t[6], t[5], is3, ALU.mult)
        tt(t[5], t[5], sl(d["Bq"], 8, 16), ALU.add)
        tt(d["B1"], t[5], t[6], ALU.subtract)
        coeff(S[2], fld(d["Gz"][1], 0), B3, d["B1"], False)
        N0 = evaluate(s, 3, LP, LQ, [hf(LM0), d["LM1"], LM2])
        parent(N0)
        Bh = hf(sl(FM, 32, 48))
        mixed(N0, fld(d["Gz"][1], 0), B3, d["B1"], Bh)
        cp(LM2, Bh)
        ts(d["g4"], Bh, 1.0, None, ALU.min)
        tt(t[3], d["g4"], fld(d["dl"], 2), ALU.mult)
        tt(hf(sl(FM, 16, 32)), t[3], fld(S[2], 3), ALU.add)
        return LP

    def lanes(s, mi, ti):
        hf = lambda t: half(t, s)
        M0 = hf(sl(FM, 0, 16))
        ts(hf(LM0), hf(mi), float(OFF), None, ALU.add)
        ts(hf(LQ1), hf(ti), 16.0, None, ALU.add)
        ts(hf(LQ2), hf(ti), 80.0, None, ALU.add)
        ts(hf(LQ3), hf(ti), 144.0, None, ALU.add)
        ts(M0, hf(mi), float(OFF), None, ALU.add)
        ts(hf(sl(FM, 48, 64)), hf(ti), float(MID), None, ALU.add)
        plus(hf(Q2e), hf(sl(FM, 48, 64)), 80.0 - MID)
        plus(hf(Q3e), hf(sl(FM, 48, 64)), 144.0 - MID)
        cg = sl(codg, 128 * s, 128 * s + 128)
        move(cg, (codw, hf(LQ1)))
        o = PS(6 + s, 0, 8)
        mm([(o, sl(SEL, 128 * a, 128 * a + 128), sl(cg, a, 128, 16), a == 0, a == 15) for a in range(16)])
        cp(hf(codi), o)
        ts(hf(w21), hf(codi), 1, None, ALU.bitwise_and)
        ts(hf(w31), hf(codi), 1, 1, ALU.logical_shift_right, ALU.bitwise_and)
        ts(hf(w32), hf(codi), 3.5, None, ALU.is_gt)
        ts(hf(C2), hf(w21), -15.0, 16.0, ALU.mult, ALU.add)
        ts(hf(U2), hf(w21), 8192.0, None, ALU.mult)
        tt(hf(U2), hf(U2), M0, ALU.add)
        ts(hf(K30), hf(codi), 1.5, None, ALU.is_lt)
        tt(hf(K30), hf(K30), M0, ALU.mult)

    N = len(T.cores)
    mi, ti = begi, taui
    for rnd in range(2):
        last = rnd == 1
        lps = []
        for s in range(2):
            tag[0] = s
            lanes(s, mi, ti)
            lps.append(search(s))
        tag[0] = None
        for a in range(16):
            ts(sl(Ew, a, 1024, 16), FM, float(-MID), dcol(a), ALU.add, ALU.mult)
        for s in range(2):
            tag[0] = s
            d = st[s]
            o = PS(4 + s, 0, 128)
            N0 = evaluate(s, 4, lps[s], None, [half(LM0, s), d["LM1"], sl(d["LPQ"], 16, 24)])
            tt(half(M3, s), d["g4"], N0, ALU.mult)
            tag[0] = None
            for f in range(4):
                k = f if f < 3 else 4
                mm([(o, sl(SELh, 128 * k, 128 * k + 128), sl(Ew, 256 * f + 128 * s, 256 * f + 128 * s + 128), f == 0, False)])
            mm([(o, SELf, sl(d["W"], 0, 128), False, True)])
            plus(sl(Rr, 128 * s, 128 * s + 128), o, rofs)
        if not last:
            ms(sl(Gw, 96, 768), 0.0)
        plus(sl(Gw, 0, 96), zer, gofs)
        ts(hh, M3, 1.0, None, ALU.min)
        scan(sc_, SEG8, hh, 0.0, ALU.mult, ALU.add)
        tt(hb, hh, neg16, ALU.mult)
        tt(hb, hb, dum16, ALU.add)
        mm([(PS(6, 0, 2), TRI1, sl(sc_, 7, 16, 8), True, False), (PS(6, 1, 2), BO, sl(sc_, 7, 8), False, True)])
        tt(a1, sc_, hb, ALU.add)
        for s in range(2):
            ts(half(Lsl, s), half(a1, s), PS(6, s, s + 1), None, ALU.add)
        cp((Gw, Lsl), Rr)
        cp(Gh, sl(Gw, 0, 96))
        mm([(("ps3", i, 381 + i, 4), sl(RSh, 128 * i, 128 * i + 128), Gh, True, True) for i in range(4)])
        wrap = lambda o, M, src: mm([(o, sl(M, 128 * q, 128 * q + 128), sl(src, q, 96, 4), q == 0, q == 3) for q in range(4)])
        wrap(PS(7, 0, 24), AQh, Gh)
        wrap(PS(6, 0, 24), ATh, Gh)
        plus(If, PS(7, 0, 24), float(MID))
        cp(LI, If)
        ts(LC, PS(6, 0, 24), c64, None, ALU.add)
        ts(rep, PS(3, 0, 384), float(MID), None, ALU.add)
        move(xc, (xw, LI))
        move(cc, (chgw, LC))
        mm([(PS(0, 0, 384), ID, xc, True, False), (PS(0, 0, 384), ID, cc, False, True)])
        act(sgn, PS(0, 0, 384), ACT.Sign, bias=-255.5)
        mm([(PS(1, 0, 384), ID, xc, True, False), (PS(1, 0, 384), ID, cc, False, False), (PS(1, 0, 384), N128I, sgn, False, True)])
        plus(new, PS(1, 0, 384), -128.0)
        pos = 0
        for j0 in range(0, 24, 3):
            lst = []
            for j in range(j0, j0 + 3):
                w = 384 - 16 * j
                e = sl(eqb, pos, pos + w)
                pos += w
                ts(e, sl(rep, 16 * j, 384), sl(If, j, j + 1), sl(wcol, j, j + 1), ALU.is_equal, ALU.mult)
                lst.append((PS(2, 16 * j, 384), BO, e, j == 0, j == 23))
            mm(lst)
        tt(dI, If, dum24, ALU.subtract)
        scan(zm, SEG4, new, 0.0, ALU.mult, ALU.max)
        scan(PS(0, 0, 384), SEG4f, PS(2, 0, 384), 0.0, ALU.mult, ALU.add)
        tt(okh, ("ps0", 3, 384, 4), thr96, ALU.is_lt)
        tt(zz, sl(zm, 3, 384, 4), okh, ALU.mult)
        cp(sl(zs, 0, 112), (zz, sl(Lout, 0, 7)))
        land = ("land%d" % rnd, 0, 112, 1)

        def send(q, rnd=rnd, land=land):
            trs = []
            for dd in range(N - 1):
                dst = T.cores[(rank + 1 + dd) % N]
                rid, pid, _ = topo.addr(dst)
                en = topo.engines(core, dst)
                k = len(en) // N
                mask = sum(1 << x for x in en[k * dd:k * dd + k])
                trs.append(RemoteDMATransfer(dst_ids=[DstId(rid=rid, pnc=pid)], dma_engine_mask=mask, remote_sem=T.sem["arr%d" % rnd],
                                             src=ap(sl(zs, 16 * dd, 16 * dd + 16)), dst=ap(sl(land, 16 * dd, 16 * dd + 16))))
            return q.remote_dma_fused(trs, local_sem=T.sem["loc%d" % rnd])
        nsig = (N - 1) * (len(topo.engines(core, T.cores[(rank + 1) % N])) // N)
        snd = add("G", send, [sl(zs, 0, 112)], [], ("raw", 1500), kind="r", hold=("raw", 600), sem=("loc%d" % rnd, nsig))
        add("X", None, [], [land], ("raw", 3500), kind="x", extra=[snd], sem=("arr%d" % rnd, nsig))
        wrap(PS(3, 0, 24), ATh, okh)
        tt(of, PS(3, 0, 24), dI, ALU.mult)
        tt(of, of, dum24, ALU.add)
        cp(Lsc, of)
        cp((xw, Lsc), new)
        move(come, (land, Lin))
        if last:
            ts(sl(Y, 0, 16), sl(FM, 0, 16), float(-OFF), -1.0, ALU.add, ALU.max)
            ts(sl(Y, 16, 32), sl(FM, 16, 32), float(-OFF), -1.0, ALU.add, ALU.max)
            tt(ml[0], sl(FM, 32, 48), hh, ALU.mult)
            ts(sl(Y, 32, 48), ml[0], float(-OFF), -1.0, ALU.add, ALU.max)
            ts(sl(Y, 48, 64), M3, float(-OFF), -1.0, ALU.add, ALU.max)
            for i in range(8):
                y = sl(Y, 8 * i, 8 * i + 8)
                dma("S", T.ym[:, 128 * i:128 * i + 128], ap(y), [y], [], 4096)
            xo = sl(xw, OFF, OFF + 1024)
            dma("S", T.yx[:], ap(xo), [xo], [], 262144)
            dma("A", T.yz[:], ap(come), [come], [], 24576)
        else:
            ts(ml[0], sl(FM, 16, 32), 1.0, None, ALU.min)
            tt(ml[1], sl(FM, 16, 32), sl(FM, 0, 16), ALU.subtract)
            tt(ml[0], ml[0], ml[1], ALU.mult)
            tt(ml[0], ml[0], sl(FM, 0, 16), ALU.add)
            tt(ml[1], M3, ml[0], ALU.subtract)
            tt(ml[1], ml[1], hh, ALU.mult)
            tt(ml[2], ml[1], ml[0], ALU.add)
            cp(Lml, ml[2])
            move(g0, (nbw, LI))
            move(hs, (swpw, LC))
            tt(sl(gd, 0, 384, 2), sl(g0, 1, 384, 2), sl(g0, 0, 384, 2), ALU.subtract)
            tt(sl(gd, 0, 384, 2), sl(gd, 0, 384, 2), sl(hs, 0, 384, 2), ALU.mult)
            times(sl(gd, 1, 384, 2), sl(gd, 0, 384, 2), -1.0)
            tt((nbw, Lsc), g0, gd, ALU.add)
            for s in (1, 0):
                hf = lambda t: half(t, s)
                xs = sl(xl, 128 * s, 128 * s + 128)
                move(xs, (xw, hf(Lml)))
                o = PS(4 + s, 0, 8)
                a0 = 12 if s == 0 else 0
                mm([(o, sl(WSEL, 128 * a, 128 * a + 128), sl(xs, a, 128, 16), a == a0, s == 1 and a == 15) for a in range(a0, 16)])
                if s == 0:
                    mm([(o, sl(WSEL, 128 * a, 128 * a + 128), sl(come, 8 * a, 8 * a + 8), False, a == 11) for a in range(12)])
                ts(hf(m0i), o, 37.0, None, ALU.mult)
                cp(hf(ui), o)
                ts(hf(ui), hf(ui), 4095, None, ALU.bitwise_and)
                tt(hf(sq), hf(ui), hf(ui), ALU.mult)
                tt(hf(m0i), hf(m0i), hf(lanef), ALU.add)
                ts(hf(sq), hf(sq), 5, 63, ALU.logical_shift_right, ALU.bitwise_and)
                ts(hf(m0i), hf(m0i), 4095, None, ALU.bitwise_and)
                tt(hf(Ti), hf(sq), hf(lanef), ALU.add)
                ts(hf(Ti), hf(Ti), 63, None, ALU.bitwise_and)
            mi, ti = m0i, Ti
    LAST["top"] = dict(top)
    return ops


def cyc(c, C):
    k, n = c
    if k == "raw":
        return n
    if k == "pe":
        return n * C["pe"]
    if k == "el":
        return max(64.0, n) + C["fix"]
    return 60.0 + n * C[k]


def replay(ops, order, eng, C):
    fin = [0.0] * len(ops)
    free = {}
    lat = C["lat"]
    for i in order:
        o = ops[i]
        e = eng[i]
        t = free.get(e, 0.0)
        for j in o["deps"]:
            x = fin[j] + (0.0 if e == "P" and eng[j] == "P" else lat)
            if x > t:
                t = x
        fin[i] = t + cyc(o["cost"][e], C)
        free[e] = t + (0.0 if e == "X" else cyc(o["hold"][e], C))
    return max(fin)


def place(ops, seq, pred, dur, hold, C, back, fixed):
    st = [0.0] * len(ops)
    fin = [0.0] * len(ops)
    eng = [None] * len(ops)
    busy = {}
    lat = C["lat"]
    for i in seq:
        best = None
        isp = "P" in dur[i]
        t0 = 0.0
        for j in pred[i]:
            x = fin[j] + (0.0 if (isp and eng[j] == "P") else lat)
            if x > t0:
                t0 = x
        for e in (dur[i] if fixed is None else (fixed[i],)):
            h = hold[i][e]
            sh = dur[i][e] - h if back else 0.0
            t = t0 + sh
            S, E = busy.setdefault(e, ([], []))
            lo, hi = 0, len(E)
            while lo < hi:
                m = (lo + hi) // 2
                if E[m] <= t:
                    lo = m + 1
                else:
                    hi = m
            while lo < len(S) and S[lo] < t + h:
                t = max(t, E[lo])
                lo += 1
            key = t - sh + dur[i][e] * (1.0 + BETA[0] if e == "V" else 1.0)
            if best is None or key < best[0]:
                best = (key, e, t, lo, h, sh)
        f, e, t, k, h, sh = best
        if h > 0:
            busy[e][0].insert(k, t)
            busy[e][1].insert(k, t + h)
        st[i] = t - sh
        fin[i] = t - sh + dur[i][e]
        eng[i] = e
    return st, fin, eng


def topo_order(ops, succ, pr):
    left = [len(o["deps"]) for o in ops]
    idx = sorted(range(len(ops)), key=lambda i: (-pr[i], i))
    out = []
    late = set()
    for i in idx:
        if left[i] > 0:
            late.add(i)
            continue
        stack = [i]
        while stack:
            a = stack.pop()
            out.append(a)
            for k in succ[a]:
                left[k] -= 1
                if left[k] == 0 and k in late:
                    late.discard(k)
                    stack.append(k)
    return out


def optimise(ops, C, lead, steps):
    n = len(ops)
    dur = [{e: cyc(c, C) for e, c in o["cost"].items()} for o in ops]
    hold = [{e: (0.0 if e == "X" else cyc(c, C)) for e, c in o["hold"].items()} for o in ops]
    pred = [o["deps"] for o in ops]
    succ = [[] for _ in range(n)]
    for i in range(n):
        for j in pred[i]:
            succ[j].append(i)
    pr = [0.0] * n
    for i in range(n - 1, -1, -1):
        pr[i] = min(dur[i].values()) + max([pr[k] + C["lat"] for k in succ[i]] + [0.0])
    pr = [pr[i] + (lead if ops[i]["tag"] == 1 else 0.0) for i in range(n)]

    def make(p):
        st, fin, eng = place(ops, topo_order(ops, succ, p), pred, dur, hold, C, False, None)
        st, fin, e2 = place(ops, sorted(range(n), key=lambda i: (-fin[i], -i)), succ, dur, hold, C, True, eng)
        st, fin, eng = place(ops, sorted(range(n), key=lambda i: (-fin[i], i)), pred, dur, hold, C, False, None)
        order = sorted(range(n), key=lambda i: (st[i], i))
        return (sum(replay(ops, order, eng, c) for c in RANGE) / len(RANGE), order, eng, st)

    best = make(pr)
    rs = np.random.RandomState(1)
    for it in range(steps):
        st = np.array(best[3])
        near = np.abs(st - rs.rand() * st.max()) < [4000.0, 10000.0][it % 2]
        p = -st + near * rs.randn(n) * [100.0, 300.0, 800.0][it % 3]
        x = make([float(v) for v in p])
        if x[0] < best[0]:
            best = x
    return best


def choose(T, rank, core, topo):
    ops = build(T, rank, core, topo, PLAN)
    lead = min(LEADS, key=lambda v: optimise(ops, COST, v, 0)[0])
    return optimise(ops, COST, lead, STEPS)


def rank_program(g, core, T, topo):
    rank = T.rank_of(core)
    if rank is None:
        return
    if "best" not in LAST:
        LAST["best"] = choose(T, rank, core, topo)
    order, eng = list(LAST["best"][1]), LAST["best"][2]
    ops = build(T, rank, core, topo, PLAN)
    for i, o in enumerate(ops):
        o["eng"] = eng[i]
    head = sorted(i for i in order if ops[i]["kind"] == "d" and not ops[i]["deps"])
    order = head + [i for i in order if i not in head]
    Q = {"V": g.vector, "A": g.scalar, "P": g.tensor, "G": g, "S": g.sync}
    pos = {}
    for k, i in enumerate(order):
        pos[i] = k
    need = {}
    marked = set()
    seen = {}
    for i in order:
        o = ops[i]
        if o["kind"] == "x":
            continue
        lat = {}
        other = []
        for j in o["deps"]:
            p = ops[j]
            if p["kind"] == "c":
                if p["eng"] == "P" and o["eng"] == "P":
                    continue
                if p["eng"] not in lat or pos[j] > pos[lat[p["eng"]]]:
                    lat[p["eng"]] = j
            else:
                other.append(j)
        w = []
        for e, j in lat.items():
            if seen.get((o["eng"], e), -1) < pos[j]:
                seen[(o["eng"], e)] = pos[j]
                marked.add(j)
                w.append(j)
        for j in other:
            if (o["eng"], j) not in seen:
                seen[(o["eng"], j)] = 1
                w.append(j)
        need[i] = w
    count = {}
    value = {}
    for i in order:
        o = ops[i]
        if o["kind"] == "c" and i in marked:
            count[o["eng"]] = count.get(o["eng"], 0) + 1
            value[i] = ("c" + o["eng"], count[o["eng"]])
        elif o["kind"] == "d":
            value[i] = (o["sem"], 16)
        elif o["kind"] in ("r", "x"):
            value[i] = o["sem"]
    waited = set()
    for i in order:
        o = ops[i]
        if o["kind"] == "x":
            continue
        q = Q[o["eng"]]
        for j in need[i]:
            q.wait_ge(T.sem[value[j][0]], value[j][1])
            waited.add(j)
        ins = o["fn"][o["eng"]](q)
        if o["kind"] == "d":
            ins.then_inc(T.sem[o["sem"]], 16)
        elif o["kind"] == "c" and i in marked:
            ins.then_inc(T.sem[value[i][0]], 1)
    for i in order:
        if ops[i]["kind"] != "c" and i not in waited:
            g.sync.wait_ge(T.sem[value[i][0]], value[i][1])
